import numpy as np
import ml_dtypes


def mxq(x, axis, fmt="e4m3"):
    dtype, down = {"e4m3": (ml_dtypes.float8_e4m3fn, 7), "e5m2": (ml_dtypes.float8_e5m2, 14)}[fmt]
    v = np.moveaxis(np.asarray(x, np.float32).astype(ml_dtypes.bfloat16).astype(np.float64), axis, -1)
    blocks = v.reshape(v.shape[:-1] + (-1, 32))
    amax = np.abs(blocks).max(-1, keepdims=True)
    byte = np.maximum(np.where(amax > 0, np.frexp(amax)[1] - 1 + 127, 0) - down, 1)
    scale = np.exp2(byte - 127.0)
    codes = (blocks / scale).astype(np.float32).astype(dtype).astype(np.float64)
    return np.moveaxis((codes * scale).reshape(v.shape), -1, axis)


WIDE = False


def mx_kscale(k):
    if not WIDE:
        return np.ones(k)
    levels = np.array([10, -10, 5, -5, 0])
    if k % 512:
        return np.exp2(np.random.permutation(np.resize(levels, k // 32))).repeat(32)
    a = np.empty((k // 512, 16))
    for p in range(k // 512):
        a[p, :8] = np.random.permutation(np.resize(levels, 8))
        for g in range(8):
            far = levels[np.abs(levels - a[p, g]) >= 10]
            a[p, g + 8] = far[np.random.randint(len(far))]
    return np.exp2(a.ravel()).repeat(32)


def f64(x):
    return np.asarray(x).astype(np.float64)


def striped(idx):
    return np.tile(np.asarray(idx).reshape(-1, 16).T, (8, 1)).astype(np.uint16)


def unstriped(offs):
    return offs[:16].T.reshape(-1).astype(np.int64)


E2M1 = np.array([0.0, 0.5, 1.0, 1.5, 2.0, 3.0, 4.0, 6.0, -0.0, -0.5, -1.0, -1.5, -2.0, -3.0, -4.0, -6.0])


def pack_weight(w, fmt):
    k, n = w.shape
    w = f64(np.asarray(w, np.float32).astype(ml_dtypes.bfloat16)).reshape(k // 32, 32, n)
    amax = np.abs(w).max(1)
    if fmt == "e4m3":
        byte = np.frexp(amax)[1] - 1 + 127 - 7
    else:
        mant, ex = np.frexp(amax / 6.0)
        byte = np.where(mant > 0.5, ex, ex - 1) + 127
    byte = np.clip(np.where(amax > 0, byte, 1), 1, 254)
    scaled = (w * np.exp2(127.0 - byte)[:, None, :]).reshape(k, n).astype(np.float32)
    by_word = np.ascontiguousarray(scaled.reshape(k // 512, 128, 4, n).transpose(0, 1, 3, 2))
    if fmt == "e4m3":
        words = by_word.astype(ml_dtypes.float8_e4m3fn).view(np.uint8)
    else:
        c = by_word.astype(ml_dtypes.float4_e2m1fn).view(np.uint8) & 0xF
        words = (c[..., 0::2] | (c[..., 1::2] << 4)).reshape(k // 512, 128, 2 * n)
    return np.ascontiguousarray(words), np.ascontiguousarray(byte.astype(np.uint8).reshape(k // 512, 16, n))


def unpack_weight(words, scales, fmt):
    g, _, n = scales.shape
    words = np.ascontiguousarray(words).reshape(g, 128, n, -1)
    if fmt == "e4m3":
        vals = words.view(ml_dtypes.float8_e4m3fn).astype(np.float64)
    else:
        nib = np.empty((g, 128, n, 4), np.uint8)
        nib[..., 0::2] = words & 0xF
        nib[..., 1::2] = words >> 4
        vals = E2M1[nib]
    vals = vals * np.repeat(np.exp2(scales.astype(np.float64) - 127.0), 8, axis=1)[..., None]
    return vals.transpose(0, 1, 3, 2).reshape(g * 512, n)


B, N, T, D, DV, NQ = 2, 512, 2048, 512, 0, 256


def setup_inputs():
    n = np.random.standard_normal
    seg = T // B
    idx = np.concatenate([b * seg + np.random.permutation(seg)[:N] for b in range(B)])
    s = mx_kscale(D)[:, None]
    kp = pack_weight(n((D, T)) / s, "e4m3")
    return {
        "qT": (n((B, D, NQ)) * s * (1.00 / np.sqrt(D))).astype(np.float32),
        "k_words": kp[0],
        "k_scales": kp[1],
        "kb": np.tile(n(T), (128, 1)).astype(np.float32),
        "offs": striped(idx),
    }


def reference(qT, k_words, k_scales, kb, offs):
    idx = unstriped(offs)
    pool = unpack_weight(k_words, k_scales, "e4m3")
    pick = lambda x: x[:, idx].reshape(x.shape[0], B, N).transpose(1, 0, 2)
    a = mxq(f64(qT), 1, "e4m3").transpose(0, 2, 1) @ pick(pool)
    a = a + pick(f64(kb))[:, :1, :]
    out = np.zeros((B, NQ, T))
    for b in range(B):
        out[b][:, idx[b * N:(b + 1) * N]] = a[b]
    return out

@@ -1,0 +1,136 @@
+from contextlib import ExitStack
+
+import concourse.mybir as mybir
+from concourse.masks import make_identity
+
+B, N, T, D, NQ = 2, 512, 2048, 512, 256
+P = 128
+PACK = 4
+SEG = T // B
+LIST_COLS = N // 16
+FLOPS = 2 * B * NQ * N * D
+
+F32 = mybir.dt.float32
+BF16 = mybir.dt.bfloat16
+I32 = mybir.dt.int32
+U32 = mybir.dt.uint32
+U16 = mybir.dt.uint16
+U8 = mybir.dt.uint8
+FP8X4 = mybir.dt.float8_e4m3fn_x4
+IDENTITY = mybir.ActivationFunctionType.Identity
+
+
+def tile_attend_sddmm_kb_seg_kernel(tc, qT, k_words, k_scales, kb, offs, out):
+    nc = tc.nc
+    slot_tiles = N // P
+    query_tiles = NQ // P
+    with ExitStack() as ctx:
+        keep = ctx.enter_context(tc.tile_pool(name="keep", bufs=1))
+        ps_t = ctx.enter_context(tc.psum_pool(name="ps_t", bufs=4))
+        ps_b = ctx.enter_context(tc.psum_pool(name="ps_b", bufs=1))
+        ps_a = ctx.enter_context(tc.psum_pool(name="ps_a", bufs=3))
+
+        offsets = keep.tile([P, B * LIST_COLS], U16, name="offsets")
+        nc.sync.dma_start(offsets[:], offs)
+
+        pool_scales = keep.tile([P, T], U8, name="pool_scales", align_bytes=64)
+        nc.vector.memset(pool_scales[:].bitcast(I32), 0)
+        for r in range(4):
+            nc.scalar.dma_start(pool_scales[r:P:32, :].bitcast(I32), k_scales[0][r:16:4, :].bitcast(I32))
+
+        pool_words = keep.tile([P, T], U32, name="pool_words", align_bytes=64)
+        pool_bias = keep.tile([P, T], F32, name="pool_bias", align_bytes=64)
+        word_bytes = k_words[0].rearrange("p n t -> p (n t)")
+        q_raw = []
+        for b in range(B):
+            seg = slice(b * SEG, (b + 1) * SEG)
+            nc.sync.dma_start(
+                pool_words[:, seg].bitcast(I32),
+                word_bytes[:, b * SEG * PACK : (b + 1) * SEG * PACK].bitcast(I32),
+            )
+            raw = keep.tile([P, PACK, NQ], F32, name=f"q_raw{b}")
+            nc.sync.dma_start(raw[:], qT[b].rearrange("(p j) w -> p j w", j=PACK))
+            q_raw.append(raw)
+            nc.sync.dma_start(pool_bias[:, seg], kb[:, seg])
+
+        rows = {}
+        for b in range(B):
+            for j in range(query_tiles):
+                row = keep.tile([P, (b + 1) * SEG], F32, name=f"row{b}{j}")
+                nc.vector.memset(row[:, b * SEG :], 0.0)
+                rows[b, j] = row
+
+        zeros = keep.tile([P, SEG], F32, name="zeros")
+        nc.scalar.copy(zeros[:], rows[0, 0][:])
+        for b in range(B):
+            other = slice((1 - b) * SEG, (2 - b) * SEG)
+            for j in range(query_tiles):
+                nc.sync.dma_start(out[b, j * P : (j + 1) * P, other], zeros[:])
+
+        ident = keep.tile([P, P], F32, name="ident")
+        make_identity(nc, ident[:])
+
+        scores = {}
+        for b in range(B):
+            entries = offsets[:, b * LIST_COLS : (b + 1) * LIST_COLS]
+            reach = slice(0, (b + 1) * SEG)
+            key_words = keep.tile([P, N], U32, name=f"key_words{b}", align_bytes=64)
+            nc.vector.tensor_copy(key_words[:], pool_words[:, reach].indirect(entries))
+            key_scales = keep.tile([P, N], U8, name=f"key_scales{b}", align_bytes=64)
+            nc.vector.tensor_copy(key_scales[:], pool_scales[:, reach].indirect(entries))
+
+            grouped = keep.tile([P, NQ, PACK], BF16, name=f"grouped{b}", align_bytes=64)
+            nc.scalar.copy(grouped[:], q_raw[b][:].rearrange("p j w -> p w j"))
+            q_words = keep.tile([P, NQ], U32, name=f"q_words{b}", align_bytes=64)
+            q_scales = keep.tile([P, NQ], U8, name=f"q_scales{b}", align_bytes=64)
+            nc.vector.quantize_mx(
+                out=q_words[:].bitcast(FP8X4),
+                scales=q_scales[:],
+                in_=grouped[:].rearrange("p w j -> p (w j)"),
+            )
+
+            key_bias = keep.tile([P, N], F32, name=f"key_bias{b}")
+            nc.vector.tensor_copy(key_bias[:], pool_bias[:, reach].indirect(entries))
+
+            banks = []
+            for h in range(slot_tiles // 2):
+                bank = ps_t.tile([P, 2, NQ], F32, name="by_slot")
+                for u in range(2):
+                    cols = slice((2 * h + u) * P, (2 * h + u + 1) * P)
+                    nc.tensor.matmul_mx(
+                        out=bank[:, u, :],
+                        lhsT=key_words[:, cols].bitcast(FP8X4),
+                        lhsT_scale=key_scales[:, cols],
+                        rhs=q_words[:].bitcast(FP8X4),
+                        rhs_scale=q_scales[:],
+                        start=True,
+                        stop=True,
+                    )
+                banks.append(bank)
+
+            bias_t = ps_b.tile([P, slot_tiles, P], F32, name="bias_t")
+            for s in range(slot_tiles):
+                nc.tensor.transpose(bias_t[:, s, :], key_bias[:, s * P : (s + 1) * P], ident[:])
+            bias_col = keep.tile([P, slot_tiles], F32, name=f"bias_col{b}")
+            nc.scalar.copy(bias_col[:], bias_t[:, :, 0])
+
+            biased = []
+            for s in range(slot_tiles):
+                tile = keep.tile([P, NQ], F32, name=f"biased{b}{s}")
+                nc.scalar.activation(tile[:], banks[s // 2][:, s % 2, :], IDENTITY, bias=bias_col[:, s : s + 1])
+                biased.append(tile)
+
+            for j in range(query_tiles):
+                turned = ps_a.tile([P, N], F32, name="by_query")
+                for s in range(slot_tiles):
+                    nc.tensor.transpose(turned[:, s * P : (s + 1) * P], biased[s][:, j * P : (j + 1) * P], ident[:])
+                score = keep.tile([P, N], F32, name=f"score{b}{j}")
+                nc.scalar.copy(score[:], turned[:])
+                scores[b, j] = score
+
+        for b in range(B):
+            entries = offsets[:, b * LIST_COLS : (b + 1) * LIST_COLS]
+            seg = slice(b * SEG, (b + 1) * SEG)
+            for j in range(query_tiles):
+                nc.vector.tensor_copy(rows[b, j][:].indirect(entries), scores[b, j][:])
+                nc.sync.dma_start(out[b, j * P : (j + 1) * P, seg], rows[b, j][:, seg])

@@ -8,6 +8,7 @@ P = 128
 PACK = 4
 SEG = T // B
 LIST_COLS = N // 16
+HEAD = 32
 FLOPS = 2 * B * NQ * N * D
 
 F32 = mybir.dt.float32
@@ -34,7 +35,7 @@ def tile_attend_sddmm_kb_seg_kernel(tc, qT, k_words, k_scales, kb, offs, out):
         nc.sync.dma_start(offsets[:], offs)
 
         pool_scales = keep.tile([P, T], U8, name="pool_scales", align_bytes=64)
-        nc.vector.memset(pool_scales[:].bitcast(I32), 0)
+        nc.gpsimd.memset(pool_scales[:].bitcast(I32), 0)
         for r in range(4):
             nc.scalar.dma_start(pool_scales[r:P:32, :].bitcast(I32), k_scales[0][r:16:4, :].bitcast(I32))
 
@@ -44,13 +45,13 @@ def tile_attend_sddmm_kb_seg_kernel(tc, qT, k_words, k_scales, kb, offs, out):
         q_raw = []
         for b in range(B):
             seg = slice(b * SEG, (b + 1) * SEG)
+            raw = keep.tile([P, PACK, NQ], F32, name=f"q_raw{b}")
+            nc.sync.dma_start(raw[:], qT[b].rearrange("(p j) w -> p j w", j=PACK))
+            q_raw.append(raw)
             nc.sync.dma_start(
                 pool_words[:, seg].bitcast(I32),
                 word_bytes[:, b * SEG * PACK : (b + 1) * SEG * PACK].bitcast(I32),
             )
-            raw = keep.tile([P, PACK, NQ], F32, name=f"q_raw{b}")
-            nc.sync.dma_start(raw[:], qT[b].rearrange("(p j) w -> p j w", j=PACK))
-            q_raw.append(raw)
             nc.sync.dma_start(pool_bias[:, seg], kb[:, seg])
 
         rows = {}
@@ -61,7 +62,8 @@ def tile_attend_sddmm_kb_seg_kernel(tc, qT, k_words, k_scales, kb, offs, out):
                 rows[b, j] = row
 
         zeros = keep.tile([P, SEG], F32, name="zeros")
-        nc.scalar.copy(zeros[:], rows[0, 0][:])
+        nc.scalar.activation(zeros[:, :HEAD], rows[0, 0][:, :HEAD], IDENTITY)
+        nc.scalar.copy(zeros[:, HEAD:], rows[1, 1][:, SEG + HEAD :])
         for b in range(B):
             other = slice((1 - b) * SEG, (2 - b) * SEG)
             for j in range(query_tiles):
@@ -74,10 +76,10 @@ def tile_attend_sddmm_kb_seg_kernel(tc, qT, k_words, k_scales, kb, offs, out):
         for b in range(B):
             entries = offsets[:, b * LIST_COLS : (b + 1) * LIST_COLS]
             reach = slice(0, (b + 1) * SEG)
-            key_words = keep.tile([P, N], U32, name=f"key_words{b}", align_bytes=64)
-            nc.vector.tensor_copy(key_words[:], pool_words[:, reach].indirect(entries))
             key_scales = keep.tile([P, N], U8, name=f"key_scales{b}", align_bytes=64)
             nc.vector.tensor_copy(key_scales[:], pool_scales[:, reach].indirect(entries))
+            key_words = keep.tile([P, N], U32, name=f"key_words{b}", align_bytes=64)
+            nc.vector.tensor_copy(key_words[:], pool_words[:, reach].indirect(entries))
 
             grouped = keep.tile([P, NQ, PACK], BF16, name=f"grouped{b}", align_bytes=64)
             nc.scalar.copy(grouped[:], q_raw[b][:].rearrange("p j w -> p w j"))
@@ -93,7 +95,7 @@ def tile_attend_sddmm_kb_seg_kernel(tc, qT, k_words, k_scales, kb, offs, out):
             nc.vector.tensor_copy(key_bias[:], pool_bias[:, reach].indirect(entries))
 
             banks = []
-            for h in range(slot_tiles // 2):
+            for h in range(2):
                 bank = ps_t.tile([P, 2, NQ], F32, name="by_slot")
                 for u in range(2):
                     cols = slice((2 * h + u) * P, (2 * h + u + 1) * P)
@@ -114,23 +116,26 @@ def tile_attend_sddmm_kb_seg_kernel(tc, qT, k_words, k_scales, kb, offs, out):
             bias_col = keep.tile([P, slot_tiles], F32, name=f"bias_col{b}")
             nc.scalar.copy(bias_col[:], bias_t[:, :, 0])
 
-            biased = []
-            for s in range(slot_tiles):
-                tile = keep.tile([P, NQ], F32, name=f"biased{b}{s}")
-                nc.scalar.activation(tile[:], banks[s // 2][:, s % 2, :], IDENTITY, bias=bias_col[:, s : s + 1])
-                biased.append(tile)
-
-            for j in range(query_tiles):
-                turned = ps_a.tile([P, N], F32, name="by_query")
-                for s in range(slot_tiles):
-                    nc.tensor.transpose(turned[:, s * P : (s + 1) * P], biased[s][:, j * P : (j + 1) * P], ident[:])
-                score = keep.tile([P, N], F32, name=f"score{b}{j}")
+            for h in range(2):
+                biased = []
+                for u in range(2):
+                    s = 2 * h + u
+                    tile = keep.tile([P, NQ], F32, name=f"biased{b}{s}")
+                    nc.scalar.activation(tile[:], banks[h][:, u, :], IDENTITY, bias=bias_col[:, s : s + 1])
+                    biased.append(tile)
+                turned = ps_a.tile([P, query_tiles, 2 * P], F32, name="by_query")
+                for j in range(query_tiles):
+                    for u in range(2):
+                        nc.tensor.transpose(turned[:, j, u * P : (u + 1) * P], biased[u][:, j * P : (j + 1) * P], ident[:])
+                score = keep.tile([P, query_tiles, 2 * P], F32, name=f"score{b}{h}")
                 nc.scalar.copy(score[:], turned[:])
-                scores[b, j] = score
+                scores[b, h] = score
 
         for b in range(B):
-            entries = offsets[:, b * LIST_COLS : (b + 1) * LIST_COLS]
             seg = slice(b * SEG, (b + 1) * SEG)
-            for j in range(query_tiles):
-                nc.vector.tensor_copy(rows[b, j][:].indirect(entries), scores[b, j][:])
-                nc.sync.dma_start(out[b, j * P : (j + 1) * P, seg], rows[b, j][:, seg])
+            for h in range(2):
+                half = offsets[:, (2 * b + h) * LIST_COLS // 2 : (2 * b + h + 1) * LIST_COLS // 2]
+                for j in range(query_tiles):
+                    nc.vector.tensor_copy(rows[b, j][:].indirect(half), scores[b, h][:, j, :])
+                    if h == 1:
+                        nc.sync.dma_start(out[b, j * P : (j + 1) * P, seg], rows[b, j][:, seg])

@@ -1,14 +1,17 @@
 from contextlib import ExitStack
 
 import concourse.mybir as mybir
-from concourse.masks import make_identity
 
 B, N, T, D, NQ = 2, 512, 2048, 512, 256
 P = 128
 PACK = 4
 SEG = T // B
 LIST_COLS = N // 16
-HEAD = 32
+ONES_COLS = PACK * NQ + 16
+BANK = 2048
+BIAS_BANK = (0, 3)
+SLOT_BANKS = ((1, 2), (2, 4))
+QUERY_BANKS = ((3, 4, 5, 6), (0, 1, 7, 5))
 FLOPS = 2 * B * NQ * N * D
 
 F32 = mybir.dt.float32
@@ -27,32 +30,55 @@ def tile_attend_sddmm_kb_seg_kernel(tc, qT, k_words, k_scales, kb, offs, out):
     query_tiles = NQ // P
     with ExitStack() as ctx:
         keep = ctx.enter_context(tc.tile_pool(name="keep", bufs=1))
-        ps_t = ctx.enter_context(tc.psum_pool(name="ps_t", bufs=4))
-        ps_b = ctx.enter_context(tc.psum_pool(name="ps_b", bufs=1))
-        ps_a = ctx.enter_context(tc.psum_pool(name="ps_a", bufs=3))
+        late = ctx.enter_context(tc.tile_pool(name="late", bufs=1))
+        psum = ctx.enter_context(tc.psum_pool(name="psum", bufs=1))
 
         offsets = keep.tile([P, B * LIST_COLS], U16, name="offsets")
         nc.sync.dma_start(offsets[:], offs)
 
         pool_scales = keep.tile([P, T], U8, name="pool_scales", align_bytes=64)
-        nc.gpsimd.memset(pool_scales[:].bitcast(I32), 0)
+        nc.vector.memset(pool_scales[:].bitcast(I32), 0)
         for r in range(4):
-            nc.scalar.dma_start(pool_scales[r:P:32, :].bitcast(I32), k_scales[0][r:16:4, :].bitcast(I32))
+            nc.sync.dma_start(pool_scales[r:P:32, :].bitcast(I32), k_scales[0][r:16:4, :].bitcast(I32))
 
-        pool_words = keep.tile([P, T], U32, name="pool_words", align_bytes=64)
-        pool_bias = keep.tile([P, T], F32, name="pool_bias", align_bytes=64)
+        ones = late.tile([P, ONES_COLS], F32, name="ones", offset=T * 4 - 32)
+        nc.vector.memset(ones[:, :P], 1.0)
+        ident = keep.tile([P, P], F32, name="ident")
+        nc.gpsimd.affine_select(
+            out=ident[:],
+            in_=ones[:, :P],
+            compare_op=mybir.AluOpType.is_equal,
+            fill=0.0,
+            base=0,
+            pattern=[[-1, P]],
+            channel_multiplier=1,
+        )
+
+        q_first = keep.tile([P, PACK, NQ], F32, name="q_first")
+        q_second = late.tile([P, PACK, NQ], F32, name="q_second", offset=T * 4)
+        pool_words = late.tile([P, T], U32, name="pool_words", offset=0)
+        pool_bias = late.tile([P, T], F32, name="pool_bias", offset=(T + PACK * NQ) * 4)
+        q_raw = [q_first, q_second]
         word_bytes = k_words[0].rearrange("p n t -> p (n t)")
-        q_raw = []
-        for b in range(B):
-            seg = slice(b * SEG, (b + 1) * SEG)
-            raw = keep.tile([P, PACK, NQ], F32, name=f"q_raw{b}")
-            nc.sync.dma_start(raw[:], qT[b].rearrange("(p j) w -> p j w", j=PACK))
-            q_raw.append(raw)
+
+        def load_queries(b):
+            nc.sync.dma_start(q_raw[b][:], qT[b].rearrange("(p j) w -> p j w", j=PACK))
+
+        def load_words(b):
             nc.sync.dma_start(
-                pool_words[:, seg].bitcast(I32),
+                pool_words[:, b * SEG : (b + 1) * SEG].bitcast(I32),
                 word_bytes[:, b * SEG * PACK : (b + 1) * SEG * PACK].bitcast(I32),
             )
-            nc.sync.dma_start(pool_bias[:, seg], kb[:, seg])
+
+        def load_bias(b):
+            nc.sync.dma_start(pool_bias[:, b * SEG : (b + 1) * SEG], kb[:, b * SEG : (b + 1) * SEG])
+
+        load_queries(0)
+        load_queries(1)
+        load_bias(0)
+        load_words(0)
+        load_bias(1)
+        load_words(1)
 
         rows = {}
         for b in range(B):
@@ -61,42 +87,48 @@ def tile_attend_sddmm_kb_seg_kernel(tc, qT, k_words, k_scales, kb, offs, out):
                 nc.vector.memset(row[:, b * SEG :], 0.0)
                 rows[b, j] = row
 
-        zeros = keep.tile([P, SEG], F32, name="zeros")
-        nc.scalar.activation(zeros[:, :HEAD], rows[0, 0][:, :HEAD], IDENTITY)
-        nc.scalar.copy(zeros[:, HEAD:], rows[1, 1][:, SEG + HEAD :])
+
+        grouped = []
+        for b in range(B):
+            rounded = keep.tile([P, NQ, PACK], BF16, name=f"grouped{b}", align_bytes=64)
+            nc.scalar.activation(rounded[:], q_raw[b][:].rearrange("p j w -> p w j"), IDENTITY)
+            grouped.append(rounded)
+
+        zeros = late.tile([P, SEG], F32, name="zeros", offset=T * 4)
+        nc.scalar.copy(zeros[:], rows[0, 0][:])
         for b in range(B):
             other = slice((1 - b) * SEG, (2 - b) * SEG)
             for j in range(query_tiles):
                 nc.sync.dma_start(out[b, j * P : (j + 1) * P, other], zeros[:])
 
-        ident = keep.tile([P, P], F32, name="ident")
-        make_identity(nc, ident[:])
-
         scores = {}
         for b in range(B):
             entries = offsets[:, b * LIST_COLS : (b + 1) * LIST_COLS]
             reach = slice(0, (b + 1) * SEG)
-            key_scales = keep.tile([P, N], U8, name=f"key_scales{b}", align_bytes=64)
-            nc.vector.tensor_copy(key_scales[:], pool_scales[:, reach].indirect(entries))
             key_words = keep.tile([P, N], U32, name=f"key_words{b}", align_bytes=64)
+            key_scales = keep.tile([P, N], U8, name=f"key_scales{b}", align_bytes=64)
+            key_bias = keep.tile([P, N], F32, name=f"key_bias{b}")
+            nc.vector.tensor_copy(key_scales[:], pool_scales[:, reach].indirect(entries))
+            nc.vector.tensor_copy(key_bias[:], pool_bias[:, reach].indirect(entries))
             nc.vector.tensor_copy(key_words[:], pool_words[:, reach].indirect(entries))
 
-            grouped = keep.tile([P, NQ, PACK], BF16, name=f"grouped{b}", align_bytes=64)
-            nc.scalar.copy(grouped[:], q_raw[b][:].rearrange("p j w -> p w j"))
             q_words = keep.tile([P, NQ], U32, name=f"q_words{b}", align_bytes=64)
             q_scales = keep.tile([P, NQ], U8, name=f"q_scales{b}", align_bytes=64)
             nc.vector.quantize_mx(
                 out=q_words[:].bitcast(FP8X4),
                 scales=q_scales[:],
-                in_=grouped[:].rearrange("p w j -> p (w j)"),
+                in_=grouped[b][:].rearrange("p w j -> p (w j)"),
             )
 
-            key_bias = keep.tile([P, N], F32, name=f"key_bias{b}")
-            nc.vector.tensor_copy(key_bias[:], pool_bias[:, reach].indirect(entries))
+            bias_t = psum.tile([P, slot_tiles, P], F32, name=f"bias_t{b}", offset=BIAS_BANK[b] * BANK)
+            for s in range(slot_tiles):
+                nc.tensor.transpose(bias_t[:, s, :], key_bias[:, s * P : (s + 1) * P], ident[:])
+            bias_col = keep.tile([P, slot_tiles], F32, name=f"bias_col{b}")
+            nc.scalar.copy(bias_col[:], bias_t[:, :, 0])
 
             banks = []
             for h in range(2):
-                bank = ps_t.tile([P, 2, NQ], F32, name="by_slot")
+                bank = psum.tile([P, 2, NQ], F32, name=f"by_slot{b}{h}", offset=SLOT_BANKS[b][h] * BANK)
                 for u in range(2):
                     cols = slice((2 * h + u) * P, (2 * h + u + 1) * P)
                     nc.tensor.matmul_mx(
@@ -110,12 +142,6 @@ def tile_attend_sddmm_kb_seg_kernel(tc, qT, k_words, k_scales, kb, offs, out):
                     )
                 banks.append(bank)
 
-            bias_t = ps_b.tile([P, slot_tiles, P], F32, name="bias_t")
-            for s in range(slot_tiles):
-                nc.tensor.transpose(bias_t[:, s, :], key_bias[:, s * P : (s + 1) * P], ident[:])
-            bias_col = keep.tile([P, slot_tiles], F32, name=f"bias_col{b}")
-            nc.scalar.copy(bias_col[:], bias_t[:, :, 0])
-
             for h in range(2):
                 biased = []
                 for u in range(2):
@@ -123,19 +149,21 @@ def tile_attend_sddmm_kb_seg_kernel(tc, qT, k_words, k_scales, kb, offs, out):
                     tile = keep.tile([P, NQ], F32, name=f"biased{b}{s}")
                     nc.scalar.activation(tile[:], banks[h][:, u, :], IDENTITY, bias=bias_col[:, s : s + 1])
                     biased.append(tile)
-                turned = ps_a.tile([P, query_tiles, 2 * P], F32, name="by_query")
                 for j in range(query_tiles):
+                    turned = psum.tile(
+                        [P, 2 * P], F32, name=f"by_query{b}{h}{j}", offset=QUERY_BANKS[b][2 * h + j] * BANK
+                    )
                     for u in range(2):
-                        nc.tensor.transpose(turned[:, j, u * P : (u + 1) * P], biased[u][:, j * P : (j + 1) * P], ident[:])
-                score = keep.tile([P, query_tiles, 2 * P], F32, name=f"score{b}{h}")
-                nc.scalar.copy(score[:], turned[:])
-                scores[b, h] = score
+                        nc.tensor.transpose(turned[:, u * P : (u + 1) * P], biased[u][:, j * P : (j + 1) * P], ident[:])
+                    score = keep.tile([P, 2 * P], F32, name=f"score{b}{h}{j}")
+                    nc.scalar.copy(score[:], turned[:])
+                    scores[b, h, j] = score
 
         for b in range(B):
             seg = slice(b * SEG, (b + 1) * SEG)
             for h in range(2):
                 half = offsets[:, (2 * b + h) * LIST_COLS // 2 : (2 * b + h + 1) * LIST_COLS // 2]
                 for j in range(query_tiles):
-                    nc.vector.tensor_copy(rows[b, j][:].indirect(half), scores[b, h][:, j, :])
+                    nc.vector.tensor_copy(rows[b, j][:].indirect(half), scores[b, h, j][:])
                     if h == 1:
                         nc.sync.dma_start(out[b, j * P : (j + 1) * P, seg], rows[b, j][:, seg])

@@ -7,7 +7,7 @@ P = 128
 PACK = 4
 SEG = T // B
 LIST_COLS = N // 16
-ONES_COLS = PACK * NQ + 16
+ONES_COLS = PACK * NQ + 2 * T + 16
 BANK = 2048
 BIAS_BANK = (0, 3)
 SLOT_BANKS = ((1, 2), (2, 4))
@@ -57,7 +57,7 @@ def tile_attend_sddmm_kb_seg_kernel(tc, qT, k_words, k_scales, kb, offs, out):
         q_first = keep.tile([P, PACK, NQ], F32, name="q_first")
         q_second = late.tile([P, PACK, NQ], F32, name="q_second", offset=T * 4)
         pool_words = late.tile([P, T], U32, name="pool_words", offset=0)
-        pool_bias = late.tile([P, T], F32, name="pool_bias", offset=(T + PACK * NQ) * 4)
+        pool_bias = late.tile([P, T], F32, name="pool_bias", offset=(3 * T + PACK * NQ) * 4)
         q_raw = [q_first, q_second]
         word_bytes = k_words[0].rearrange("p n t -> p (n t)")
 
@@ -81,12 +81,14 @@ def tile_attend_sddmm_kb_seg_kernel(tc, qT, k_words, k_scales, kb, offs, out):
         load_words(1)
 
         rows = {}
-        for b in range(B):
-            for j in range(query_tiles):
-                row = keep.tile([P, (b + 1) * SEG], F32, name=f"row{b}{j}")
-                nc.vector.memset(row[:, b * SEG :], 0.0)
-                rows[b, j] = row
-
+        for j in range(query_tiles):
+            row = keep.tile([P, SEG], F32, name=f"row0{j}")
+            nc.vector.memset(row[:].bitcast(I32), 0)
+            rows[0, j] = row
+        for j in range(query_tiles):
+            row = late.tile([P, T], F32, name=f"row1{j}", offset=((1 + j) * T + PACK * NQ) * 4)
+            nc.gpsimd.memset(row[:, SEG:], 0.0)
+            rows[1, j] = row
 
         grouped = []
         for b in range(B):

@@ -7,11 +7,6 @@ P = 128
 PACK = 4
 SEG = T // B
 LIST_COLS = N // 16
-ONES_COLS = PACK * NQ + 2 * T + 16
-BANK = 2048
-BIAS_BANK = (0, 3)
-SLOT_BANKS = ((1, 2), (2, 4))
-QUERY_BANKS = ((3, 4, 5, 6), (0, 1, 7, 5))
 FLOPS = 2 * B * NQ * N * D
 
 F32 = mybir.dt.float32
@@ -22,150 +17,115 @@ U16 = mybir.dt.uint16
 U8 = mybir.dt.uint8
 FP8X4 = mybir.dt.float8_e4m3fn_x4
 IDENTITY = mybir.ActivationFunctionType.Identity
+ADD = mybir.AluOpType.add
+
+KIB = 1024
 
 
 def tile_attend_sddmm_kb_seg_kernel(tc, qT, k_words, k_scales, kb, offs, out):
     nc = tc.nc
-    slot_tiles = N // P
     query_tiles = NQ // P
     with ExitStack() as ctx:
         keep = ctx.enter_context(tc.tile_pool(name="keep", bufs=1))
-        late = ctx.enter_context(tc.tile_pool(name="late", bufs=1))
+        shared = ctx.enter_context(tc.tile_pool(name="shared", bufs=1))
         psum = ctx.enter_context(tc.psum_pool(name="psum", bufs=1))
 
         offsets = keep.tile([P, B * LIST_COLS], U16, name="offsets")
         nc.sync.dma_start(offsets[:], offs)
+        entries = [offsets[:, b * LIST_COLS : (b + 1) * LIST_COLS] for b in range(B)]
+        segs = [slice(b * SEG, (b + 1) * SEG) for b in range(B)]
 
-        pool_scales = keep.tile([P, T], U8, name="pool_scales", align_bytes=64)
+        pool_scales = shared.tile([P, T], U8, name="pool_scales", offset=32 * KIB, align_bytes=64)
         nc.vector.memset(pool_scales[:].bitcast(I32), 0)
-        for r in range(4):
-            nc.sync.dma_start(pool_scales[r:P:32, :].bitcast(I32), k_scales[0][r:16:4, :].bitcast(I32))
 
-        ones = late.tile([P, ONES_COLS], F32, name="ones", offset=T * 4 - 32)
-        nc.vector.memset(ones[:, :P], 1.0)
-        ident = keep.tile([P, P], F32, name="ident")
-        nc.gpsimd.affine_select(
-            out=ident[:],
-            in_=ones[:, :P],
-            compare_op=mybir.AluOpType.is_equal,
-            fill=0.0,
-            base=0,
-            pattern=[[-1, P]],
-            channel_multiplier=1,
-        )
+        all_words = k_words[0].rearrange("p n t -> p (n t)").bitcast(I32)
 
-        q_first = keep.tile([P, PACK, NQ], F32, name="q_first")
-        q_second = late.tile([P, PACK, NQ], F32, name="q_second", offset=T * 4)
-        pool_words = late.tile([P, T], U32, name="pool_words", offset=0)
-        pool_bias = late.tile([P, T], F32, name="pool_bias", offset=(3 * T + PACK * NQ) * 4)
-        q_raw = [q_first, q_second]
-        word_bytes = k_words[0].rearrange("p n t -> p (n t)")
+        def load_words(b, offset):
+            window = shared.tile([P, (b + 1) * SEG], U32, name=f"pool_words{b}", offset=offset)
+            nc.sync.dma_start(window[:, segs[b]].bitcast(I32), all_words[:, segs[b]])
+            return window
 
-        def load_queries(b):
-            nc.sync.dma_start(q_raw[b][:], qT[b].rearrange("(p j) w -> p j w", j=PACK))
+        def gather_words(b, window, offset):
+            words = shared.tile([P, N], U32, name=f"key_words{b}", offset=offset, align_bytes=64)
+            nc.vector.tensor_copy(words[:], window[:].indirect(entries[b]))
+            return words
 
-        def load_words(b):
-            nc.sync.dma_start(
-                pool_words[:, b * SEG : (b + 1) * SEG].bitcast(I32),
-                word_bytes[:, b * SEG * PACK : (b + 1) * SEG * PACK].bitcast(I32),
-            )
+        def load_queries(b, offset):
+            raw = shared.tile([P, PACK, NQ], F32, name=f"q_raw{b}", offset=offset)
+            nc.sync.dma_start(raw[:], qT[b].rearrange("(p j) w -> p j w", j=PACK))
+            return raw
 
-        def load_bias(b):
-            nc.sync.dma_start(pool_bias[:, b * SEG : (b + 1) * SEG], kb[:, b * SEG : (b + 1) * SEG])
-
-        load_queries(0)
-        load_queries(1)
-        load_bias(0)
-        load_words(0)
-        load_bias(1)
-        load_words(1)
-
-        rows = {}
-        for j in range(query_tiles):
-            row = keep.tile([P, SEG], F32, name=f"row0{j}")
-            nc.vector.memset(row[:].bitcast(I32), 0)
-            rows[0, j] = row
-        for j in range(query_tiles):
-            row = late.tile([P, T], F32, name=f"row1{j}", offset=((1 + j) * T + PACK * NQ) * 4)
-            nc.gpsimd.memset(row[:, SEG:], 0.0)
-            rows[1, j] = row
-
-        grouped = []
-        for b in range(B):
-            rounded = keep.tile([P, NQ, PACK], BF16, name=f"grouped{b}", align_bytes=64)
-            nc.scalar.activation(rounded[:], q_raw[b][:].rearrange("p j w -> p w j"), IDENTITY)
-            grouped.append(rounded)
-
-        zeros = late.tile([P, SEG], F32, name="zeros", offset=T * 4)
-        nc.scalar.copy(zeros[:], rows[0, 0][:])
-        for b in range(B):
-            other = slice((1 - b) * SEG, (2 - b) * SEG)
-            for j in range(query_tiles):
-                nc.sync.dma_start(out[b, j * P : (j + 1) * P, other], zeros[:])
-
-        scores = {}
-        for b in range(B):
-            entries = offsets[:, b * LIST_COLS : (b + 1) * LIST_COLS]
-            reach = slice(0, (b + 1) * SEG)
-            key_words = keep.tile([P, N], U32, name=f"key_words{b}", align_bytes=64)
-            key_scales = keep.tile([P, N], U8, name=f"key_scales{b}", align_bytes=64)
-            key_bias = keep.tile([P, N], F32, name=f"key_bias{b}")
-            nc.vector.tensor_copy(key_scales[:], pool_scales[:, reach].indirect(entries))
-            nc.vector.tensor_copy(key_bias[:], pool_bias[:, reach].indirect(entries))
-            nc.vector.tensor_copy(key_words[:], pool_words[:, reach].indirect(entries))
-
-            q_words = keep.tile([P, NQ], U32, name=f"q_words{b}", align_bytes=64)
+        def quantise(b, raw):
+            rounded = shared.tile([P, NQ, PACK], BF16, name=f"grouped{b}", offset=(24 + 2 * b) * KIB, align_bytes=64)
+            nc.scalar.activation(rounded[:], raw[:].rearrange("p j w -> p w j"), IDENTITY)
+            q_words = shared.tile([P, NQ], U32, name=f"q_words{b}", offset=(32 + b) * KIB, align_bytes=64)
             q_scales = keep.tile([P, NQ], U8, name=f"q_scales{b}", align_bytes=64)
             nc.vector.quantize_mx(
                 out=q_words[:].bitcast(FP8X4),
                 scales=q_scales[:],
-                in_=grouped[b][:].rearrange("p w j -> p (w j)"),
+                in_=rounded[:].rearrange("p w j -> p (w j)"),
             )
+            return q_words, q_scales
 
-            bias_t = psum.tile([P, slot_tiles, P], F32, name=f"bias_t{b}", offset=BIAS_BANK[b] * BANK)
-            for s in range(slot_tiles):
-                nc.tensor.transpose(bias_t[:, s, :], key_bias[:, s * P : (s + 1) * P], ident[:])
-            bias_col = keep.tile([P, slot_tiles], F32, name=f"bias_col{b}")
-            nc.scalar.copy(bias_col[:], bias_t[:, :, 0])
+        def load_bias(b):
+            window = shared.tile([P, (b + 1) * SEG], F32, name=f"pool_bias{b}", offset=12 * KIB)
+            nc.sync.dma_start(window[:, segs[b]], kb[:, segs[b]])
+            return window
 
-            banks = []
-            for h in range(2):
-                bank = psum.tile([P, 2, NQ], F32, name=f"by_slot{b}{h}", offset=SLOT_BANKS[b][h] * BANK)
-                for u in range(2):
-                    cols = slice((2 * h + u) * P, (2 * h + u + 1) * P)
-                    nc.tensor.matmul_mx(
-                        out=bank[:, u, :],
-                        lhsT=key_words[:, cols].bitcast(FP8X4),
-                        lhsT_scale=key_scales[:, cols],
-                        rhs=q_words[:].bitcast(FP8X4),
-                        rhs_scale=q_scales[:],
-                        start=True,
-                        stop=True,
-                    )
-                banks.append(bank)
+        def gather_bias(b, window, offset):
+            bias = shared.tile([P, N], F32, name=f"key_bias{b}", offset=offset, align_bytes=64)
+            nc.vector.tensor_copy(bias[:], window[:].indirect(entries[b]))
+            return bias
 
-            for h in range(2):
-                biased = []
-                for u in range(2):
-                    s = 2 * h + u
-                    tile = keep.tile([P, NQ], F32, name=f"biased{b}{s}")
-                    nc.scalar.activation(tile[:], banks[h][:, u, :], IDENTITY, bias=bias_col[:, s : s + 1])
-                    biased.append(tile)
-                for j in range(query_tiles):
-                    turned = psum.tile(
-                        [P, 2 * P], F32, name=f"by_query{b}{h}{j}", offset=QUERY_BANKS[b][2 * h + j] * BANK
-                    )
-                    for u in range(2):
-                        nc.tensor.transpose(turned[:, u * P : (u + 1) * P], biased[u][:, j * P : (j + 1) * P], ident[:])
-                    score = keep.tile([P, 2 * P], F32, name=f"score{b}{h}{j}")
-                    nc.scalar.copy(score[:], turned[:])
-                    scores[b, h, j] = score
+        window0 = load_words(0, 6 * KIB)
+        bias0 = load_bias(0)
+        raw0 = load_queries(0, 20 * KIB)
+        for r in range(4):
+            nc.sync.dma_start(pool_scales[r:P:32, :].bitcast(I32), k_scales[0][r:16:4, :].bitcast(I32))
 
+        rows = {}
+        for b, j in ((0, 0), (1, 0), (1, 1)):
+            row = keep.tile([P, (b + 1) * SEG], F32, name=f"row{b}{j}")
+            nc.vector.memset(row[:, segs[b]].bitcast(I32), 0)
+            rows[b, j] = row
+        rows[0, 1] = rows[0, 0]
+
+        key_words = [gather_words(0, window0, 30 * KIB)]
+        key_bias = [gather_bias(0, bias0, 28 * KIB)]
+        key_scales = keep.tile([P, B * N], U8, name="key_scales", align_bytes=64)
+        nc.vector.tensor_copy(key_scales[:], pool_scales[:].indirect(offsets[:]))
+        queries = [quantise(0, raw0)]
+
+        window1 = load_words(1, 0)
+        raw1 = load_queries(1, 8 * KIB)
+        bias1 = load_bias(1)
+
+        key_words.append(gather_words(1, window1, 24 * KIB))
+        queries.append(quantise(1, raw1))
+        key_bias.append(gather_bias(1, bias1, 26 * KIB))
+
+        zeros = keep.tile([P, SEG], F32, name="zeros")
+        nc.scalar.copy(zeros[:], rows[1, 1][:, SEG:])
         for b in range(B):
-            seg = slice(b * SEG, (b + 1) * SEG)
-            for h in range(2):
-                half = offsets[:, (2 * b + h) * LIST_COLS // 2 : (2 * b + h + 1) * LIST_COLS // 2]
-                for j in range(query_tiles):
-                    nc.vector.tensor_copy(rows[b, j][:].indirect(half), scores[b, h, j][:])
-                    if h == 1:
-                        nc.sync.dma_start(out[b, j * P : (j + 1) * P, seg], rows[b, j][:, seg])
+            for j in range(query_tiles):
+                nc.sync.dma_start(out[b, j * P : (j + 1) * P, segs[1 - b]], zeros[:])
+
+        for j in range(query_tiles):
+            cols = slice(j * P, (j + 1) * P)
+            for b in range(B):
+                slots = slice(b * N, (b + 1) * N)
+                q_words, q_scales = queries[b]
+                bank = psum.tile([P, N], F32, name=f"bank{b}{j}", offset=((0, 1), (1, 2))[b][j] * 2 * KIB)
+                nc.tensor.matmul_mx(
+                    out=bank[:],
+                    lhsT=q_words[:, cols].bitcast(FP8X4),
+                    lhsT_scale=q_scales[:, cols],
+                    rhs=key_words[b][:].bitcast(FP8X4),
+                    rhs_scale=key_scales[:, slots],
+                    start=True,
+                    stop=True,
+                )
+                score = keep.tile([P, N], F32, name=f"score{b}{j}")
+                nc.scalar.copy(score[:], bank[:])
+                nc.vector.tensor_tensor(rows[b, j][:].indirect(entries[b]), score[:], key_bias[b][:], ADD)
+                nc.sync.dma_start(out[b, j * P : (j + 1) * P, segs[b]], rows[b, j][:, segs[b]])

@@ -77,18 +77,15 @@ def tile_attend_sddmm_kb_seg_kernel(tc, qT, k_words, k_scales, kb, offs, out):
             nc.vector.tensor_copy(bias[:], window[:].indirect(entries[b]))
             return bias
 
-        window0 = load_words(0, 6 * KIB)
+        window0 = load_words(0, 0)
         bias0 = load_bias(0)
         raw0 = load_queries(0, 20 * KIB)
         for r in range(4):
             nc.sync.dma_start(pool_scales[r:P:32, :].bitcast(I32), k_scales[0][r:16:4, :].bitcast(I32))
 
-        rows = {}
-        for b, j in ((0, 0), (1, 0), (1, 1)):
-            row = keep.tile([P, (b + 1) * SEG], F32, name=f"row{b}{j}")
-            nc.vector.memset(row[:, segs[b]].bitcast(I32), 0)
-            rows[b, j] = row
-        rows[0, 1] = rows[0, 0]
+        row0 = keep.tile([P, SEG], F32, name="row0")
+        nc.vector.memset(row0[:].bitcast(I32), 0)
+        rows = {(0, 0): row0, (0, 1): row0}
 
         key_words = [gather_words(0, window0, 30 * KIB)]
         key_bias = [gather_bias(0, bias0, 28 * KIB)]
@@ -97,35 +94,42 @@ def tile_attend_sddmm_kb_seg_kernel(tc, qT, k_words, k_scales, kb, offs, out):
         queries = [quantise(0, raw0)]
 
         window1 = load_words(1, 0)
-        raw1 = load_queries(1, 8 * KIB)
+        raw1 = load_queries(1, 20 * KIB)
         bias1 = load_bias(1)
 
         key_words.append(gather_words(1, window1, 24 * KIB))
         queries.append(quantise(1, raw1))
         key_bias.append(gather_bias(1, bias1, 26 * KIB))
 
-        zeros = keep.tile([P, SEG], F32, name="zeros")
-        nc.scalar.copy(zeros[:], rows[1, 1][:, SEG:])
+        zeros = shared.tile([P, SEG], F32, name="zeros", offset=0)
+        nc.gpsimd.memset(zeros[:], 0.0)
+        for j, offset in enumerate((4 * KIB, 12 * KIB)):
+            row = shared.tile([P, T], F32, name=f"row1{j}", offset=offset)
+            nc.gpsimd.memset(row[:, SEG:], 0.0)
+            rows[1, j] = row
         for b in range(B):
             for j in range(query_tiles):
                 nc.sync.dma_start(out[b, j * P : (j + 1) * P, segs[1 - b]], zeros[:])
 
-        for j in range(query_tiles):
+        for b, j in ((0, 0), (1, 0), (1, 1), (0, 1)):
             cols = slice(j * P, (j + 1) * P)
-            for b in range(B):
-                slots = slice(b * N, (b + 1) * N)
+            if True:
                 q_words, q_scales = queries[b]
-                bank = psum.tile([P, N], F32, name=f"bank{b}{j}", offset=((0, 1), (1, 2))[b][j] * 2 * KIB)
-                nc.tensor.matmul_mx(
-                    out=bank[:],
-                    lhsT=q_words[:, cols].bitcast(FP8X4),
-                    lhsT_scale=q_scales[:, cols],
-                    rhs=key_words[b][:].bitcast(FP8X4),
-                    rhs_scale=key_scales[:, slots],
-                    start=True,
-                    stop=True,
-                )
                 score = keep.tile([P, N], F32, name=f"score{b}{j}")
-                nc.scalar.copy(score[:], bank[:])
+                for h in range(2):
+                    half = slice(h * N // 2, (h + 1) * N // 2)
+                    slots = slice(b * N + half.start, b * N + half.stop)
+                    first_bank = 2 * ((0, 2), (1, 2))[b][j]
+                    bank = psum.tile([P, N // 2], F32, name=f"bank{b}{j}{h}", offset=(first_bank + h) * 2 * KIB)
+                    nc.tensor.matmul_mx(
+                        out=bank[:],
+                        lhsT=q_words[:, cols].bitcast(FP8X4),
+                        lhsT_scale=q_scales[:, cols],
+                        rhs=key_words[b][:, half].bitcast(FP8X4),
+                        rhs_scale=key_scales[:, slots],
+                        start=True,
+                        stop=True,
+                    )
+                    nc.scalar.copy(score[:, half], bank[:])
                 nc.vector.tensor_tensor(rows[b, j][:].indirect(entries[b]), score[:], key_bias[b][:], ADD)
                 nc.sync.dma_start(out[b, j * P : (j + 1) * P, segs[b]], rows[b, j][:, segs[b]])

@@ -20,6 +20,8 @@ IDENTITY = mybir.ActivationFunctionType.Identity
 ADD = mybir.AluOpType.add
 
 KIB = 1024
+BANK = 2 * KIB
+PER_PARTITION = T // P
 
 
 def tile_attend_sddmm_kb_seg_kernel(tc, qT, k_words, k_scales, kb, offs, out):
@@ -34,31 +36,49 @@ def tile_attend_sddmm_kb_seg_kernel(tc, qT, k_words, k_scales, kb, offs, out):
         nc.sync.dma_start(offsets[:], offs)
         entries = [offsets[:, b * LIST_COLS : (b + 1) * LIST_COLS] for b in range(B)]
         segs = [slice(b * SEG, (b + 1) * SEG) for b in range(B)]
-
-        pool_scales = shared.tile([P, T], U8, name="pool_scales", offset=32 * KIB, align_bytes=64)
-        nc.vector.memset(pool_scales[:].bitcast(I32), 0)
-
         all_words = k_words[0].rearrange("p n t -> p (n t)").bitcast(I32)
 
-        def load_words(b, offset):
-            window = shared.tile([P, (b + 1) * SEG], U32, name=f"pool_words{b}", offset=offset)
-            nc.sync.dma_start(window[:, segs[b]].bitcast(I32), all_words[:, segs[b]])
-            return window
+        bias_down = keep.tile([P, PER_PARTITION], F32, name="bias_down")
+        nc.sync.dma_start(bias_down[:], kb[0].rearrange("(p c) -> p c", p=P))
+        words0 = keep.tile([P, SEG], U32, name="pool_words0")
+        nc.sync.dma_start(words0[:].bitcast(I32), all_words[:, segs[0]])
 
-        def gather_words(b, window, offset):
-            words = shared.tile([P, N], U32, name=f"key_words{b}", offset=offset, align_bytes=64)
+        pool_scales = keep.tile([P, T], U8, name="pool_scales", align_bytes=64)
+        nc.vector.memset(pool_scales[:].bitcast(I32), 0)
+        for r in range(4):
+            nc.sync.dma_start(pool_scales[r:P:32, :].bitcast(I32), k_scales[0][r:16:4, :].bitcast(I32))
+
+        ones = shared.tile([P, P], F32, name="ones", offset=8 * KIB - 256)
+        nc.vector.memset(ones[:], 1.0)
+        ident = keep.tile([P, P], F32, name="ident")
+        nc.gpsimd.affine_select(
+            out=ident[:],
+            in_=ones[:],
+            compare_op=mybir.AluOpType.is_equal,
+            fill=0.0,
+            base=0,
+            pattern=[[-1, P]],
+            channel_multiplier=1,
+        )
+
+        raw = shared.tile([P, B, PACK, NQ], F32, name="q_raw", offset=0)
+        for b in range(B):
+            nc.sync.dma_start(raw[:, b], qT[b].rearrange("(p j) w -> p j w", j=PACK))
+        words1 = shared.tile([P, T], U32, name="pool_words1", offset=8 * KIB)
+        nc.sync.dma_start(words1[:, segs[1]].bitcast(I32), all_words[:, segs[1]])
+
+        first_rows = keep.tile([P, T], F32, name="first_rows")
+        nc.vector.memset(first_rows[:].bitcast(I32), 0)
+
+        def gather_words(b, window):
+            words = keep.tile([P, N], U32, name=f"key_words{b}", align_bytes=64)
             nc.vector.tensor_copy(words[:], window[:].indirect(entries[b]))
             return words
 
-        def load_queries(b, offset):
-            raw = shared.tile([P, PACK, NQ], F32, name=f"q_raw{b}", offset=offset)
-            nc.sync.dma_start(raw[:], qT[b].rearrange("(p j) w -> p j w", j=PACK))
-            return raw
-
-        def quantise(b, raw):
-            rounded = shared.tile([P, NQ, PACK], BF16, name=f"grouped{b}", offset=(24 + 2 * b) * KIB, align_bytes=64)
-            nc.scalar.activation(rounded[:], raw[:].rearrange("p j w -> p w j"), IDENTITY)
-            q_words = shared.tile([P, NQ], U32, name=f"q_words{b}", offset=(32 + b) * KIB, align_bytes=64)
+        def quantise(b):
+            rounded = keep.tile([P, NQ, PACK], BF16, name=f"grouped{b}", align_bytes=64)
+            nc.scalar.activation(rounded[:], raw[:, b].rearrange("p j w -> p w j"), IDENTITY)
+            q_words = keep.tile([P, NQ], U32, name=f"q_words{b}", align_bytes=64)
             q_scales = keep.tile([P, NQ], U8, name=f"q_scales{b}", align_bytes=64)
             nc.vector.quantize_mx(
                 out=q_words[:].bitcast(FP8X4),
@@ -67,69 +87,60 @@ def tile_attend_sddmm_kb_seg_kernel(tc, qT, k_words, k_scales, kb, offs, out):
             )
             return q_words, q_scales
 
-        def load_bias(b):
-            window = shared.tile([P, (b + 1) * SEG], F32, name=f"pool_bias{b}", offset=12 * KIB)
-            nc.sync.dma_start(window[:, segs[b]], kb[:, segs[b]])
-            return window
-
-        def gather_bias(b, window, offset):
-            bias = shared.tile([P, N], F32, name=f"key_bias{b}", offset=offset, align_bytes=64)
-            nc.vector.tensor_copy(bias[:], window[:].indirect(entries[b]))
-            return bias
-
-        window0 = load_words(0, 0)
-        bias0 = load_bias(0)
-        raw0 = load_queries(0, 20 * KIB)
-        for r in range(4):
-            nc.sync.dma_start(pool_scales[r:P:32, :].bitcast(I32), k_scales[0][r:16:4, :].bitcast(I32))
-
-        row0 = keep.tile([P, SEG], F32, name="row0")
-        nc.vector.memset(row0[:].bitcast(I32), 0)
-        rows = {(0, 0): row0, (0, 1): row0}
-
-        key_words = [gather_words(0, window0, 30 * KIB)]
-        key_bias = [gather_bias(0, bias0, 28 * KIB)]
+        key_words = [gather_words(0, words0)]
         key_scales = keep.tile([P, B * N], U8, name="key_scales", align_bytes=64)
         nc.vector.tensor_copy(key_scales[:], pool_scales[:].indirect(offsets[:]))
-        queries = [quantise(0, raw0)]
+        queries = [quantise(0)]
+        key_words.append(gather_words(1, words1))
+        queries.append(quantise(1))
 
-        window1 = load_words(1, 0)
-        raw1 = load_queries(1, 20 * KIB)
-        bias1 = load_bias(1)
+        pool_bias = shared.tile([P, T], F32, name="pool_bias", offset=24 * KIB)
+        by_group = pool_bias[:].rearrange("q (p g i) -> q g p i", g=PER_PARTITION // 4, i=4)
+        for g in range(PER_PARTITION // 4):
+            spread = psum.tile([P, 4, P], F32, name=f"spread{g}", offset=(4 + g) * BANK)
+            for i in range(4):
+                c = 4 * g + i
+                nc.tensor.transpose(spread[:, i, :], bias_down[:, c : c + 1].to_broadcast([P, P]), ident[:])
+            nc.scalar.copy(by_group[:, g], spread[:].rearrange("q i p -> q p i"))
 
-        key_words.append(gather_words(1, window1, 24 * KIB))
-        queries.append(quantise(1, raw1))
-        key_bias.append(gather_bias(1, bias1, 26 * KIB))
+        key_bias = shared.tile([P, B * N], F32, name="key_bias", offset=0)
+        nc.vector.tensor_copy(key_bias[:], pool_bias[:].indirect(offsets[:]))
 
-        zeros = shared.tile([P, SEG], F32, name="zeros", offset=0)
+        zeros = shared.tile([P, SEG], F32, name="zeros", offset=22 * KIB)
         nc.gpsimd.memset(zeros[:], 0.0)
-        for j, offset in enumerate((4 * KIB, 12 * KIB)):
-            row = shared.tile([P, T], F32, name=f"row1{j}", offset=offset)
-            nc.gpsimd.memset(row[:, SEG:], 0.0)
-            rows[1, j] = row
         for b in range(B):
             for j in range(query_tiles):
                 nc.sync.dma_start(out[b, j * P : (j + 1) * P, segs[1 - b]], zeros[:])
+        second_rows = []
+        for b, offset in enumerate((26 * KIB, 30 * KIB)):
+            row = shared.tile([P, (b + 1) * SEG], F32, name=f"second_rows{b}", offset=offset)
+            nc.gpsimd.memset(row[:, segs[b]], 0.0)
+            second_rows.append(row)
 
-        for b, j in ((0, 0), (1, 0), (1, 1), (0, 1)):
+        scores = []
+        for j in range(query_tiles):
             cols = slice(j * P, (j + 1) * P)
-            if True:
+            score = keep.tile([P, B * N], F32, name=f"score{j}")
+            for b in range(B):
+                slots = slice(b * N, (b + 1) * N)
                 q_words, q_scales = queries[b]
-                score = keep.tile([P, N], F32, name=f"score{b}{j}")
-                for h in range(2):
-                    half = slice(h * N // 2, (h + 1) * N // 2)
-                    slots = slice(b * N + half.start, b * N + half.stop)
-                    first_bank = 2 * ((0, 2), (1, 2))[b][j]
-                    bank = psum.tile([P, N // 2], F32, name=f"bank{b}{j}{h}", offset=(first_bank + h) * 2 * KIB)
-                    nc.tensor.matmul_mx(
-                        out=bank[:],
-                        lhsT=q_words[:, cols].bitcast(FP8X4),
-                        lhsT_scale=q_scales[:, cols],
-                        rhs=key_words[b][:, half].bitcast(FP8X4),
-                        rhs_scale=key_scales[:, slots],
-                        start=True,
-                        stop=True,
-                    )
-                    nc.scalar.copy(score[:, half], bank[:])
-                nc.vector.tensor_tensor(rows[b, j][:].indirect(entries[b]), score[:], key_bias[b][:], ADD)
-                nc.sync.dma_start(out[b, j * P : (j + 1) * P, segs[b]], rows[b, j][:, segs[b]])
+                bank = psum.tile([P, N], F32, name=f"bank{b}{j}", offset=(B * j + b) * BANK)
+                nc.tensor.matmul_mx(
+                    out=bank[:],
+                    lhsT=q_words[:, cols].bitcast(FP8X4),
+                    lhsT_scale=q_scales[:, cols],
+                    rhs=key_words[b][:].bitcast(FP8X4),
+                    rhs_scale=key_scales[:, slots],
+                    start=True,
+                    stop=True,
+                )
+                nc.scalar.copy(score[:, slots], bank[:])
+            scores.append(score)
+
+        nc.vector.tensor_tensor(first_rows[:].indirect(offsets[:]), scores[0][:], key_bias[:], ADD)
+        for b in range(B):
+            nc.sync.dma_start(out[b, :P, segs[b]], first_rows[:, segs[b]])
+        for b in range(B):
+            slots = slice(b * N, (b + 1) * N)
+            nc.vector.tensor_tensor(second_rows[b][:].indirect(entries[b]), scores[1][:, slots], key_bias[:, slots], ADD)
+            nc.sync.dma_start(out[b, P:, segs[b]], second_rows[b][:, segs[b]])

@@ -43,13 +43,14 @@ def tile_attend_sddmm_kb_seg_kernel(tc, qT, k_words, k_scales, kb, offs, out):
         words0 = keep.tile([P, SEG], U32, name="pool_words0")
         nc.sync.dma_start(words0[:].bitcast(I32), all_words[:, segs[0]])
 
+        ones = shared.tile([P, P], F32, name="ones", offset=8 * KIB - 256)
+        nc.vector.memset(ones[:], 1.0)
+
         pool_scales = keep.tile([P, T], U8, name="pool_scales", align_bytes=64)
         nc.vector.memset(pool_scales[:].bitcast(I32), 0)
         for r in range(4):
             nc.sync.dma_start(pool_scales[r:P:32, :].bitcast(I32), k_scales[0][r:16:4, :].bitcast(I32))
 
-        ones = shared.tile([P, P], F32, name="ones", offset=8 * KIB - 256)
-        nc.vector.memset(ones[:], 1.0)
         ident = keep.tile([P, P], F32, name="ident")
         nc.gpsimd.affine_select(
             out=ident[:],
@@ -143,4 +144,6 @@ def tile_attend_sddmm_kb_seg_kernel(tc, qT, k_words, k_scales, kb, offs, out):
         for b in range(B):
             slots = slice(b * N, (b + 1) * N)
             nc.vector.tensor_tensor(second_rows[b][:].indirect(entries[b]), scores[1][:, slots], key_bias[:, slots], ADD)
-            nc.sync.dma_start(out[b, P:, segs[b]], second_rows[b][:, segs[b]])
+            for queue, start in ((nc.sync, b * SEG), (nc.scalar, b * SEG + SEG // 2)):
+                half = slice(start, start + SEG // 2)
+                queue.dma_start(out[b, P:, half], second_rows[b][:, half])

@@ -7,6 +7,7 @@ P = 128
 PACK = 4
 SEG = T // B
 LIST_COLS = N // 16
+SCALE_ROWS = D // 32
 FLOPS = 2 * B * NQ * N * D
 
 F32 = mybir.dt.float32
@@ -22,11 +23,11 @@ ADD = mybir.AluOpType.add
 KIB = 1024
 BANK = 2 * KIB
 PER_PARTITION = T // P
+RAW_AT = (8 * KIB + 512, 16 * KIB)
 
 
 def tile_attend_sddmm_kb_seg_kernel(tc, qT, k_words, k_scales, kb, offs, out):
     nc = tc.nc
-    query_tiles = NQ // P
     with ExitStack() as ctx:
         keep = ctx.enter_context(tc.tile_pool(name="keep", bufs=1))
         shared = ctx.enter_context(tc.tile_pool(name="shared", bufs=1))
@@ -36,25 +37,35 @@ def tile_attend_sddmm_kb_seg_kernel(tc, qT, k_words, k_scales, kb, offs, out):
         nc.sync.dma_start(offsets[:], offs)
         entries = [offsets[:, b * LIST_COLS : (b + 1) * LIST_COLS] for b in range(B)]
         segs = [slice(b * SEG, (b + 1) * SEG) for b in range(B)]
+        slots = [slice(b * N, (b + 1) * N) for b in range(B)]
         all_words = k_words[0].rearrange("p n t -> p (n t)").bitcast(I32)
 
-        bias_down = keep.tile([P, PER_PARTITION], F32, name="bias_down")
-        nc.sync.dma_start(bias_down[:], kb[0].rearrange("(p c) -> p c", p=P))
-        words0 = keep.tile([P, SEG], U32, name="pool_words0")
-        nc.sync.dma_start(words0[:].bitcast(I32), all_words[:, segs[0]])
-
-        ones = shared.tile([P, P], F32, name="ones", offset=8 * KIB - 256)
-        nc.vector.memset(ones[:], 1.0)
-
         pool_scales = keep.tile([P, T], U8, name="pool_scales", align_bytes=64)
-        nc.vector.memset(pool_scales[:].bitcast(I32), 0)
-        for r in range(4):
-            nc.sync.dma_start(pool_scales[r:P:32, :].bitcast(I32), k_scales[0][r:16:4, :].bitcast(I32))
+        held = B * SCALE_ROWS
+        nc.sync.dma_start(
+            pool_scales[:held, SEG:].bitcast(I32),
+            k_scales[0].rearrange("f (b t) -> (f b) t", b=B).bitcast(I32),
+        )
+        nc.vector.memset(pool_scales[held : 2 * held, SEG:].bitcast(I32), 0)
+        nc.vector.memset(pool_scales[2 * held :, SEG:].bitcast(I32), 0)
+
+        bias_down = shared.tile([P, PER_PARTITION], F32, name="bias_down", offset=28 * KIB)
+        nc.sync.dma_start(bias_down[:], kb[0].rearrange("(p c) -> p c", p=P))
+
+        pool_words, raw = [], []
+        for b in range(B):
+            words = keep.tile([P, (b + 1) * SEG], U32, name=f"pool_words{b}")
+            nc.sync.dma_start(words[:, segs[b]].bitcast(I32), all_words[:, segs[b]])
+            pool_words.append(words)
+            rows = shared.tile([P, PACK, NQ], F32, name=f"q_raw{b}", offset=RAW_AT[b])
+            nc.sync.dma_start(rows[:], qT[b].rearrange("(p j) w -> p j w", j=PACK))
+            raw.append(rows)
 
         ident = keep.tile([P, P], F32, name="ident")
+        nc.gpsimd.memset(ident[:], 1.0)
         nc.gpsimd.affine_select(
             out=ident[:],
-            in_=ones[:],
+            in_=ident[:],
             compare_op=mybir.AluOpType.is_equal,
             fill=0.0,
             base=0,
@@ -62,23 +73,32 @@ def tile_attend_sddmm_kb_seg_kernel(tc, qT, k_words, k_scales, kb, offs, out):
             channel_multiplier=1,
         )
 
-        raw = shared.tile([P, B, PACK, NQ], F32, name="q_raw", offset=0)
+        key_scales = []
         for b in range(B):
-            nc.sync.dma_start(raw[:, b], qT[b].rearrange("(p j) w -> p j w", j=PACK))
-        words1 = shared.tile([P, T], U32, name="pool_words1", offset=8 * KIB)
-        nc.sync.dma_start(words1[:, segs[1]].bitcast(I32), all_words[:, segs[1]])
+            plane = keep.tile([P, N], U8, name=f"key_scales{b}", align_bytes=64)
+            nc.vector.memset(plane[:].bitcast(I32), 0)
+            key_scales.append(plane)
+        first_row = keep.tile([P, SEG], F32, name="first_row")
+        nc.vector.memset(first_row[:].bitcast(I32), 0)
 
-        first_rows = keep.tile([P, T], F32, name="first_rows")
-        nc.vector.memset(first_rows[:].bitcast(I32), 0)
+        for b in range(B):
+            window = pool_scales[:, (1 - b) * SEG :]
+            picked = keep.tile([P, N], U8, name=f"picked_scales{b}", align_bytes=64)
+            nc.vector.tensor_copy(picked[:], window.indirect(entries[b]))
+            for r in range(4):
+                nc.sync.dma_start(
+                    key_scales[b][r:P:32, :].bitcast(I32),
+                    picked[B * r + b : held : 4 * B, :].bitcast(I32),
+                )
 
-        def gather_words(b, window):
+        key_words = []
+        for b in range(B):
             words = keep.tile([P, N], U32, name=f"key_words{b}", align_bytes=64)
-            nc.vector.tensor_copy(words[:], window[:].indirect(entries[b]))
-            return words
+            nc.vector.tensor_copy(words[:], pool_words[b][:].indirect(entries[b]))
+            key_words.append(words)
 
-        def quantise(b):
-            rounded = keep.tile([P, NQ, PACK], BF16, name=f"grouped{b}", align_bytes=64)
-            nc.scalar.activation(rounded[:], raw[:, b].rearrange("p j w -> p w j"), IDENTITY)
+        def quantise(b, rounded):
+            nc.scalar.activation(rounded[:], raw[b][:].rearrange("p j w -> p w j"), IDENTITY)
             q_words = keep.tile([P, NQ], U32, name=f"q_words{b}", align_bytes=64)
             q_scales = keep.tile([P, NQ], U8, name=f"q_scales{b}", align_bytes=64)
             nc.vector.quantize_mx(
@@ -88,14 +108,7 @@ def tile_attend_sddmm_kb_seg_kernel(tc, qT, k_words, k_scales, kb, offs, out):
             )
             return q_words, q_scales
 
-        key_words = [gather_words(0, words0)]
-        key_scales = keep.tile([P, B * N], U8, name="key_scales", align_bytes=64)
-        nc.vector.tensor_copy(key_scales[:], pool_scales[:].indirect(offsets[:]))
-        queries = [quantise(0)]
-        key_words.append(gather_words(1, words1))
-        queries.append(quantise(1))
-
-        pool_bias = shared.tile([P, T], F32, name="pool_bias", offset=24 * KIB)
+        pool_bias = keep.tile([P, T], F32, name="pool_bias")
         by_group = pool_bias[:].rearrange("q (p g i) -> q g p i", g=PER_PARTITION // 4, i=4)
         for g in range(PER_PARTITION // 4):
             spread = psum.tile([P, 4, P], F32, name=f"spread{g}", offset=(4 + g) * BANK)
@@ -104,46 +117,55 @@ def tile_attend_sddmm_kb_seg_kernel(tc, qT, k_words, k_scales, kb, offs, out):
                 nc.tensor.transpose(spread[:, i, :], bias_down[:, c : c + 1].to_broadcast([P, P]), ident[:])
             nc.scalar.copy(by_group[:, g], spread[:].rearrange("q i p -> q p i"))
 
-        key_bias = shared.tile([P, B * N], F32, name="key_bias", offset=0)
+        rounded0 = shared.tile([P, NQ, PACK], BF16, name="rounded0", offset=28 * KIB, align_bytes=64)
+        queries = [quantise(0, rounded0)]
+        key_bias = shared.tile([P, B * N], F32, name="key_bias", offset=12 * KIB)
         nc.vector.tensor_copy(key_bias[:], pool_bias[:].indirect(offsets[:]))
+        rounded1 = shared.tile([P, NQ, PACK], BF16, name="rounded1", offset=7 * KIB, align_bytes=64)
+        queries.append(quantise(1, rounded1))
 
-        zeros = shared.tile([P, SEG], F32, name="zeros", offset=22 * KIB)
-        nc.gpsimd.memset(zeros[:], 0.0)
-        for b in range(B):
-            for j in range(query_tiles):
-                nc.sync.dma_start(out[b, j * P : (j + 1) * P, segs[1 - b]], zeros[:])
-        second_rows = []
-        for b, offset in enumerate((26 * KIB, 30 * KIB)):
-            row = shared.tile([P, (b + 1) * SEG], F32, name=f"second_rows{b}", offset=offset)
-            nc.gpsimd.memset(row[:, segs[b]], 0.0)
-            second_rows.append(row)
-
-        scores = []
-        for j in range(query_tiles):
+        def product(b, j, score):
             cols = slice(j * P, (j + 1) * P)
-            score = keep.tile([P, B * N], F32, name=f"score{j}")
-            for b in range(B):
-                slots = slice(b * N, (b + 1) * N)
-                q_words, q_scales = queries[b]
-                bank = psum.tile([P, N], F32, name=f"bank{b}{j}", offset=(B * j + b) * BANK)
-                nc.tensor.matmul_mx(
-                    out=bank[:],
-                    lhsT=q_words[:, cols].bitcast(FP8X4),
-                    lhsT_scale=q_scales[:, cols],
-                    rhs=key_words[b][:].bitcast(FP8X4),
-                    rhs_scale=key_scales[:, slots],
-                    start=True,
-                    stop=True,
-                )
-                nc.scalar.copy(score[:, slots], bank[:])
-            scores.append(score)
+            q_words, q_scales = queries[b]
+            bank = psum.tile([P, N], F32, name=f"bank{b}{j}", offset=(B * b + j) * BANK)
+            nc.tensor.matmul_mx(
+                out=bank[:],
+                lhsT=q_words[:, cols].bitcast(FP8X4),
+                lhsT_scale=q_scales[:, cols],
+                rhs=key_words[b][:].bitcast(FP8X4),
+                rhs_scale=key_scales[b][:],
+                start=True,
+                stop=True,
+            )
+            nc.scalar.copy(score, bank[:])
 
-        nc.vector.tensor_tensor(first_rows[:].indirect(offsets[:]), scores[0][:], key_bias[:], ADD)
+        first_score = shared.tile([P, N], F32, name="first_score", offset=16 * KIB)
+        middle_score = keep.tile([P, B * N], F32, name="middle_score")
+        last_score = keep.tile([P, N], F32, name="last_score")
+        product(0, 0, first_score[:])
+        product(0, 1, middle_score[:, slots[0]])
+        product(1, 0, middle_score[:, slots[1]])
+        product(1, 1, last_score[:])
+
+        middle_rows = shared.tile([P, T], F32, name="middle_rows", offset=0)
+        nc.gpsimd.memset(middle_rows[:], 0.0)
+        zeros = shared.tile([P, SEG], F32, name="zeros", offset=8 * KIB)
+        nc.gpsimd.memset(zeros[:], 0.0)
+
+        nc.vector.tensor_tensor(first_row[:].indirect(entries[0]), first_score[:], key_bias[:, slots[0]], ADD)
+        nc.sync.dma_start(out[0, :P, segs[0]], first_row[:])
         for b in range(B):
-            nc.sync.dma_start(out[b, :P, segs[b]], first_rows[:, segs[b]])
-        for b in range(B):
-            slots = slice(b * N, (b + 1) * N)
-            nc.vector.tensor_tensor(second_rows[b][:].indirect(entries[b]), scores[1][:, slots], key_bias[:, slots], ADD)
-            for queue, start in ((nc.sync, b * SEG), (nc.scalar, b * SEG + SEG // 2)):
-                half = slice(start, start + SEG // 2)
-                queue.dma_start(out[b, P:, half], second_rows[b][:, half])
+            for j in range(NQ // P):
+                nc.sync.dma_start(out[b, j * P : (j + 1) * P, segs[1 - b]], zeros[:])
+
+        last_row = shared.tile([P, T], F32, name="last_row", offset=17 * KIB)
+        nc.gpsimd.memset(last_row[:, segs[1]], 0.0)
+
+        nc.vector.tensor_tensor(middle_rows[:].indirect(offsets[:]), middle_score[:], key_bias[:], ADD)
+        nc.sync.dma_start(out[0, P:, segs[0]], middle_rows[:, segs[0]])
+        nc.sync.dma_start(out[1, :P, segs[1]], middle_rows[:, segs[1]])
+
+        nc.vector.tensor_tensor(last_row[:].indirect(entries[1]), last_score[:], key_bias[:, slots[1]], ADD)
+        for queue, start in ((nc.sync, SEG), (nc.scalar, SEG + SEG // 2)):
+            half = slice(start, start + SEG // 2)
+            queue.dma_start(out[1, P:, half], last_row[:, half])

@@ -22,7 +22,7 @@ ADD = mybir.AluOpType.add
 
 KIB = 1024
 BANK = 2 * KIB
-PER_PARTITION = T // P
+PER_PARTITION = SEG // P
 RAW_AT = (8 * KIB + 512, 16 * KIB)
 
 
@@ -49,8 +49,11 @@ def tile_attend_sddmm_kb_seg_kernel(tc, qT, k_words, k_scales, kb, offs, out):
         nc.vector.memset(pool_scales[held : 2 * held, SEG:].bitcast(I32), 0)
         nc.vector.memset(pool_scales[2 * held :, SEG:].bitcast(I32), 0)
 
-        bias_down = shared.tile([P, PER_PARTITION], F32, name="bias_down", offset=28 * KIB)
-        nc.sync.dma_start(bias_down[:], kb[0].rearrange("(p c) -> p c", p=P))
+        bias_down = []
+        for b in range(B):
+            down = shared.tile([P, PER_PARTITION], F32, name=f"bias_down{b}", offset=(28 + 2 * b) * KIB)
+            nc.sync.dma_start(down[:], kb[0, segs[b]].rearrange("(p c) -> p c", p=P))
+            bias_down.append(down)
 
         pool_words, raw = [], []
         for b in range(B):
@@ -76,7 +79,6 @@ def tile_attend_sddmm_kb_seg_kernel(tc, qT, k_words, k_scales, kb, offs, out):
         key_scales = []
         for b in range(B):
             plane = keep.tile([P, N], U8, name=f"key_scales{b}", align_bytes=64)
-            nc.vector.memset(plane[:].bitcast(I32), 0)
             key_scales.append(plane)
         first_row = keep.tile([P, SEG], F32, name="first_row")
         nc.vector.memset(first_row[:].bitcast(I32), 0)
@@ -98,7 +100,11 @@ def tile_attend_sddmm_kb_seg_kernel(tc, qT, k_words, k_scales, kb, offs, out):
             key_words.append(words)
 
         def quantise(b, rounded):
-            nc.scalar.activation(rounded[:], raw[b][:].rearrange("p j w -> p w j"), IDENTITY)
+            nc.scalar.activation(
+                rounded[:].rearrange("p (c i) j -> p c j i", i=4),
+                raw[b][:].rearrange("p j (c i) -> p c j i", i=4),
+                IDENTITY,
+            )
             q_words = keep.tile([P, NQ], U32, name=f"q_words{b}", align_bytes=64)
             q_scales = keep.tile([P, NQ], U8, name=f"q_scales{b}", align_bytes=64)
             nc.vector.quantize_mx(
@@ -108,19 +114,24 @@ def tile_attend_sddmm_kb_seg_kernel(tc, qT, k_words, k_scales, kb, offs, out):
             )
             return q_words, q_scales
 
-        pool_bias = keep.tile([P, T], F32, name="pool_bias")
-        by_group = pool_bias[:].rearrange("q (p g i) -> q g p i", g=PER_PARTITION // 4, i=4)
-        for g in range(PER_PARTITION // 4):
-            spread = psum.tile([P, 4, P], F32, name=f"spread{g}", offset=(4 + g) * BANK)
-            for i in range(4):
-                c = 4 * g + i
-                nc.tensor.transpose(spread[:, i, :], bias_down[:, c : c + 1].to_broadcast([P, P]), ident[:])
-            nc.scalar.copy(by_group[:, g], spread[:].rearrange("q i p -> q p i"))
+        pool_bias = []
+        groups = PER_PARTITION // 4
+        for b in range(B):
+            spread_rows = keep.tile([P, (b + 1) * SEG], F32, name=f"pool_bias{b}")
+            pool_bias.append(spread_rows)
+            by_group = spread_rows[:, segs[b]].rearrange("q (p g i) -> q g p i", g=groups, i=4)
+            for g in range(groups):
+                spread = psum.tile([P, 4, P], F32, name=f"spread{b}{g}", offset=(4 + groups * b + g) * BANK)
+                for i in range(4):
+                    c = 4 * g + i
+                    nc.tensor.transpose(spread[:, i, :], bias_down[b][:, c : c + 1].to_broadcast([P, P]), ident[:])
+                nc.scalar.copy(by_group[:, g], spread[:].rearrange("q i p -> q p i"))
 
         rounded0 = shared.tile([P, NQ, PACK], BF16, name="rounded0", offset=28 * KIB, align_bytes=64)
         queries = [quantise(0, rounded0)]
         key_bias = shared.tile([P, B * N], F32, name="key_bias", offset=12 * KIB)
-        nc.vector.tensor_copy(key_bias[:], pool_bias[:].indirect(offsets[:]))
+        for b in range(B):
+            nc.vector.tensor_copy(key_bias[:, slots[b]], pool_bias[b][:].indirect(entries[b]))
         rounded1 = shared.tile([P, NQ, PACK], BF16, name="rounded1", offset=7 * KIB, align_bytes=64)
         queries.append(quantise(1, rounded1))
 

@@ -23,7 +23,7 @@ ADD = mybir.AluOpType.add
 KIB = 1024
 BANK = 2 * KIB
 PER_PARTITION = SEG // P
-RAW_AT = (8 * KIB + 512, 16 * KIB)
+RAW_AT = (16 * KIB, 28 * KIB)
 
 
 def tile_attend_sddmm_kb_seg_kernel(tc, qT, k_words, k_scales, kb, offs, out):
@@ -43,15 +43,14 @@ def tile_attend_sddmm_kb_seg_kernel(tc, qT, k_words, k_scales, kb, offs, out):
         pool_scales = keep.tile([P, T], U8, name="pool_scales", align_bytes=64)
         held = B * SCALE_ROWS
         nc.sync.dma_start(
-            pool_scales[:held, SEG:].bitcast(I32),
+            pool_scales[P - held :, SEG:].bitcast(I32),
             k_scales[0].rearrange("f (b t) -> (f b) t", b=B).bitcast(I32),
         )
-        nc.vector.memset(pool_scales[held : 2 * held, SEG:].bitcast(I32), 0)
-        nc.vector.memset(pool_scales[2 * held :, SEG:].bitcast(I32), 0)
+        nc.vector.memset(pool_scales[: P - held, SEG:].bitcast(I32), 0)
 
         bias_down = []
         for b in range(B):
-            down = shared.tile([P, PER_PARTITION], F32, name=f"bias_down{b}", offset=(28 + 2 * b) * KIB)
+            down = shared.tile([P, PER_PARTITION], F32, name=f"bias_down{b}", offset=(38 + 2 * b) * KIB)
             nc.sync.dma_start(down[:], kb[0, segs[b]].rearrange("(p c) -> p c", p=P))
             bias_down.append(down)
 
@@ -90,14 +89,14 @@ def tile_attend_sddmm_kb_seg_kernel(tc, qT, k_words, k_scales, kb, offs, out):
             for r in range(4):
                 nc.sync.dma_start(
                     key_scales[b][r:P:32, :].bitcast(I32),
-                    picked[B * r + b : held : 4 * B, :].bitcast(I32),
+                    picked[P - held + B * r + b : P : 4 * B, :].bitcast(I32),
                 )
 
-        key_words = []
-        for b in range(B):
-            words = keep.tile([P, N], U32, name=f"key_words{b}", align_bytes=64)
-            nc.vector.tensor_copy(words[:], pool_words[b][:].indirect(entries[b]))
-            key_words.append(words)
+        key_words = [
+            keep.tile([P, N], U32, name="key_words0", align_bytes=64),
+            shared.tile([P, N], U32, name="key_words1", offset=17 * KIB, align_bytes=64),
+        ]
+        nc.vector.tensor_copy(key_words[0][:], pool_words[0][:].indirect(entries[0]))
 
         def quantise(b, rounded):
             nc.scalar.activation(
@@ -114,12 +113,14 @@ def tile_attend_sddmm_kb_seg_kernel(tc, qT, k_words, k_scales, kb, offs, out):
             )
             return q_words, q_scales
 
-        pool_bias = []
+        pool_bias = [
+            keep.tile([P, SEG], F32, name="pool_bias0"),
+            shared.tile([P, T], F32, name="pool_bias1", offset=19 * KIB + 512),
+        ]
         groups = PER_PARTITION // 4
-        for b in range(B):
-            spread_rows = keep.tile([P, (b + 1) * SEG], F32, name=f"pool_bias{b}")
-            pool_bias.append(spread_rows)
-            by_group = spread_rows[:, segs[b]].rearrange("q (p g i) -> q g p i", g=groups, i=4)
+
+        def spread_bias(b):
+            by_group = pool_bias[b][:, segs[b]].rearrange("q (p g i) -> q g p i", g=groups, i=4)
             for g in range(groups):
                 spread = psum.tile([P, 4, P], F32, name=f"spread{b}{g}", offset=(4 + groups * b + g) * BANK)
                 for i in range(4):
@@ -127,12 +128,15 @@ def tile_attend_sddmm_kb_seg_kernel(tc, qT, k_words, k_scales, kb, offs, out):
                     nc.tensor.transpose(spread[:, i, :], bias_down[b][:, c : c + 1].to_broadcast([P, P]), ident[:])
                 nc.scalar.copy(by_group[:, g], spread[:].rearrange("q i p -> q p i"))
 
-        rounded0 = shared.tile([P, NQ, PACK], BF16, name="rounded0", offset=28 * KIB, align_bytes=64)
+        spread_bias(0)
+        rounded0 = shared.tile([P, NQ, PACK], BF16, name="rounded0", offset=38 * KIB, align_bytes=64)
+        key_bias = keep.tile([P, B * N], F32, name="key_bias")
+        nc.vector.tensor_copy(key_bias[:, slots[0]], pool_bias[0][:].indirect(entries[0]))
         queries = [quantise(0, rounded0)]
-        key_bias = shared.tile([P, B * N], F32, name="key_bias", offset=12 * KIB)
-        for b in range(B):
-            nc.vector.tensor_copy(key_bias[:, slots[b]], pool_bias[b][:].indirect(entries[b]))
-        rounded1 = shared.tile([P, NQ, PACK], BF16, name="rounded1", offset=7 * KIB, align_bytes=64)
+        spread_bias(1)
+        nc.vector.tensor_copy(key_words[1][:], pool_words[1][:].indirect(entries[1]))
+        nc.vector.tensor_copy(key_bias[:, slots[1]], pool_bias[1][:].indirect(entries[1]))
+        rounded1 = shared.tile([P, NQ, PACK], BF16, name="rounded1", offset=14 * KIB + 512, align_bytes=64)
         queries.append(quantise(1, rounded1))
 
         def product(b, j, score):
@@ -150,7 +154,7 @@ def tile_attend_sddmm_kb_seg_kernel(tc, qT, k_words, k_scales, kb, offs, out):
             )
             nc.scalar.copy(score, bank[:])
 
-        first_score = shared.tile([P, N], F32, name="first_score", offset=16 * KIB)
+        first_score = shared.tile([P, N], F32, name="first_score", offset=28 * KIB)
         middle_score = keep.tile([P, B * N], F32, name="middle_score")
         last_score = keep.tile([P, N], F32, name="last_score")
         product(0, 0, first_score[:])
@@ -158,9 +162,9 @@ def tile_attend_sddmm_kb_seg_kernel(tc, qT, k_words, k_scales, kb, offs, out):
         product(1, 0, middle_score[:, slots[1]])
         product(1, 1, last_score[:])
 
-        middle_rows = shared.tile([P, T], F32, name="middle_rows", offset=0)
+        middle_rows = shared.tile([P, T], F32, name="middle_rows", offset=7 * KIB)
         nc.gpsimd.memset(middle_rows[:], 0.0)
-        zeros = shared.tile([P, SEG], F32, name="zeros", offset=8 * KIB)
+        zeros = shared.tile([P, SEG], F32, name="zeros", offset=15 * KIB)
         nc.gpsimd.memset(zeros[:], 0.0)
 
         nc.vector.tensor_tensor(first_row[:].indirect(entries[0]), first_score[:], key_bias[:, slots[0]], ADD)
@@ -169,7 +173,7 @@ def tile_attend_sddmm_kb_seg_kernel(tc, qT, k_words, k_scales, kb, offs, out):
             for j in range(NQ // P):
                 nc.sync.dma_start(out[b, j * P : (j + 1) * P, segs[1 - b]], zeros[:])
 
-        last_row = shared.tile([P, T], F32, name="last_row", offset=17 * KIB)
+        last_row = shared.tile([P, T], F32, name="last_row", offset=29 * KIB)
         nc.gpsimd.memset(last_row[:, segs[1]], 0.0)
 
         nc.vector.tensor_tensor(middle_rows[:].indirect(offsets[:]), middle_score[:], key_bias[:], ADD)

@@ -154,33 +154,32 @@ def tile_attend_sddmm_kb_seg_kernel(tc, qT, k_words, k_scales, kb, offs, out):
             )
             nc.scalar.copy(score, bank[:])
 
-        first_score = shared.tile([P, N], F32, name="first_score", offset=28 * KIB)
-        middle_score = keep.tile([P, B * N], F32, name="middle_score")
-        last_score = keep.tile([P, N], F32, name="last_score")
-        product(0, 0, first_score[:])
-        product(0, 1, middle_score[:, slots[0]])
-        product(1, 0, middle_score[:, slots[1]])
-        product(1, 1, last_score[:])
+        tiles = [(b, j) for b in range(B) for j in range(NQ // P)]
+        scores = [shared.tile([P, N], F32, name="score0", offset=28 * KIB)]
+        scores.extend(keep.tile([P, N], F32, name=f"score{t}") for t in range(1, len(tiles)))
+        for (b, j), score in zip(tiles, scores):
+            product(b, j, score[:])
 
-        middle_rows = shared.tile([P, T], F32, name="middle_rows", offset=7 * KIB)
-        nc.gpsimd.memset(middle_rows[:], 0.0)
-        zeros = shared.tile([P, SEG], F32, name="zeros", offset=15 * KIB)
-        nc.gpsimd.memset(zeros[:], 0.0)
-
-        nc.vector.tensor_tensor(first_row[:].indirect(entries[0]), first_score[:], key_bias[:, slots[0]], ADD)
-        nc.sync.dma_start(out[0, :P, segs[0]], first_row[:])
-        for b in range(B):
-            for j in range(NQ // P):
-                nc.sync.dma_start(out[b, j * P : (j + 1) * P, segs[1 - b]], zeros[:])
-
-        last_row = shared.tile([P, T], F32, name="last_row", offset=29 * KIB)
+        second_row = shared.tile([P, SEG], F32, name="second_row", offset=11 * KIB)
+        nc.gpsimd.memset(second_row[:], 0.0)
+        last_row = shared.tile([P, T], F32, name="last_row", offset=15 * KIB)
         nc.gpsimd.memset(last_row[:, segs[1]], 0.0)
+        for b, j in tiles:
+            nc.scalar.dma_start(out[b, j * P : (j + 1) * P, segs[1 - b]], last_row[:, segs[1]])
 
-        nc.vector.tensor_tensor(middle_rows[:].indirect(offsets[:]), middle_score[:], key_bias[:], ADD)
-        nc.sync.dma_start(out[0, P:, segs[0]], middle_rows[:, segs[0]])
-        nc.sync.dma_start(out[1, :P, segs[1]], middle_rows[:, segs[1]])
+        def scatter(t, row):
+            b = tiles[t][0]
+            nc.vector.tensor_tensor(row[:].indirect(entries[b]), scores[t][:], key_bias[:, slots[b]], ADD)
 
-        nc.vector.tensor_tensor(last_row[:].indirect(entries[1]), last_score[:], key_bias[:, slots[1]], ADD)
+        scatter(0, first_row)
+        nc.sync.dma_start(out[0, :P, segs[0]], first_row[:])
+        third_row = shared.tile([P, T], F32, name="third_row", offset=29 * KIB)
+        nc.gpsimd.memset(third_row[:, segs[1]], 0.0)
+        scatter(1, second_row)
+        nc.sync.dma_start(out[0, P:, segs[0]], second_row[:])
+        scatter(2, third_row)
+        nc.sync.dma_start(out[1, :P, segs[1]], third_row[:, segs[1]])
+        scatter(3, last_row)
         for queue, start in ((nc.sync, SEG), (nc.scalar, SEG + SEG // 2)):
             half = slice(start, start + SEG // 2)
             queue.dma_start(out[1, P:, half], last_row[:, half])

@@ -180,6 +180,4 @@ def tile_attend_sddmm_kb_seg_kernel(tc, qT, k_words, k_scales, kb, offs, out):
         scatter(2, third_row)
         nc.sync.dma_start(out[1, :P, segs[1]], third_row[:, segs[1]])
         scatter(3, last_row)
-        for queue, start in ((nc.sync, SEG), (nc.scalar, SEG + SEG // 2)):
-            half = slice(start, start + SEG // 2)
-            queue.dma_start(out[1, P:, half], last_row[:, half])
+        nc.sync.dma_start(out[1, P:, segs[1]], last_row[:, segs[1]])

@@ -23,7 +23,7 @@ ADD = mybir.AluOpType.add
 KIB = 1024
 BANK = 2 * KIB
 PER_PARTITION = SEG // P
-RAW_AT = (16 * KIB, 28 * KIB)
+RAW_AT = (16 * KIB, 56 * KIB)
 
 
 def tile_attend_sddmm_kb_seg_kernel(tc, qT, k_words, k_scales, kb, offs, out):
@@ -93,7 +93,7 @@ def tile_attend_sddmm_kb_seg_kernel(tc, qT, k_words, k_scales, kb, offs, out):
                 )
 
         key_words = [
-            keep.tile([P, N], U32, name="key_words0", align_bytes=64),
+            shared.tile([P, N], U32, name="key_words0", offset=44 * KIB, align_bytes=64),
             shared.tile([P, N], U32, name="key_words1", offset=17 * KIB, align_bytes=64),
         ]
         nc.vector.tensor_copy(key_words[0][:], pool_words[0][:].indirect(entries[0]))
@@ -136,10 +136,8 @@ def tile_attend_sddmm_kb_seg_kernel(tc, qT, k_words, k_scales, kb, offs, out):
         spread_bias(1)
         nc.vector.tensor_copy(key_words[1][:], pool_words[1][:].indirect(entries[1]))
         nc.vector.tensor_copy(key_bias[:, slots[1]], pool_bias[1][:].indirect(entries[1]))
-        rounded1 = shared.tile([P, NQ, PACK], BF16, name="rounded1", offset=14 * KIB + 512, align_bytes=64)
-        queries.append(quantise(1, rounded1))
 
-        def product(b, j, score):
+        def product(b, j):
             cols = slice(j * P, (j + 1) * P)
             q_words, q_scales = queries[b]
             bank = psum.tile([P, N], F32, name=f"bank{b}{j}", offset=(B * b + j) * BANK)
@@ -152,32 +150,38 @@ def tile_attend_sddmm_kb_seg_kernel(tc, qT, k_words, k_scales, kb, offs, out):
                 start=True,
                 stop=True,
             )
-            nc.scalar.copy(score, bank[:])
+            return bank
 
-        tiles = [(b, j) for b in range(B) for j in range(NQ // P)]
-        scores = [shared.tile([P, N], F32, name="score0", offset=28 * KIB)]
-        scores.extend(keep.tile([P, N], F32, name=f"score{t}") for t in range(1, len(tiles)))
-        for (b, j), score in zip(tiles, scores):
-            product(b, j, score[:])
+        def scatter(b, j, score, row):
+            nc.vector.tensor_tensor(row[:].indirect(entries[b]), score[:], key_bias[:, slots[b]], ADD)
+            nc.sync.dma_start(out[b, j * P : (j + 1) * P, segs[b]], row[:, segs[b]])
 
-        second_row = shared.tile([P, SEG], F32, name="second_row", offset=11 * KIB)
+        scores = [
+            keep.tile([P, N], F32, name="score0"),
+            shared.tile([P, N], F32, name="score1", offset=RAW_AT[1]),
+            keep.tile([P, N], F32, name="score2"),
+            keep.tile([P, N], F32, name="score3"),
+        ]
+        banks = [product(0, 0), product(0, 1)]
+        nc.scalar.copy(scores[0][:], banks[0][:])
+        second_row = shared.tile([P, SEG], F32, name="second_row", offset=20 * KIB)
         nc.gpsimd.memset(second_row[:], 0.0)
-        last_row = shared.tile([P, T], F32, name="last_row", offset=15 * KIB)
-        nc.gpsimd.memset(last_row[:, segs[1]], 0.0)
-        for b, j in tiles:
-            nc.scalar.dma_start(out[b, j * P : (j + 1) * P, segs[1 - b]], last_row[:, segs[1]])
+        zeros = shared.tile([P, SEG], F32, name="zeros", offset=24 * KIB)
+        nc.gpsimd.memset(zeros[:], 0.0)
 
-        def scatter(t, row):
-            b = tiles[t][0]
-            nc.vector.tensor_tensor(row[:].indirect(entries[b]), scores[t][:], key_bias[:, slots[b]], ADD)
-
-        scatter(0, first_row)
-        nc.sync.dma_start(out[0, :P, segs[0]], first_row[:])
-        third_row = shared.tile([P, T], F32, name="third_row", offset=29 * KIB)
+        scatter(0, 0, scores[0], first_row)
+        rounded1 = shared.tile([P, NQ, PACK], BF16, name="rounded1", offset=44 * KIB, align_bytes=64)
+        queries.append(quantise(1, rounded1))
+        nc.scalar.copy(scores[1][:], banks[1][:])
+        for b in range(B):
+            for j in range(NQ // P):
+                nc.scalar.dma_start(out[b, j * P : (j + 1) * P, segs[1 - b]], zeros[:])
+        for j in range(NQ // P):
+            nc.scalar.copy(scores[2 + j][:], product(1, j)[:])
+        third_row = shared.tile([P, T], F32, name="third_row", offset=37 * KIB)
         nc.gpsimd.memset(third_row[:, segs[1]], 0.0)
-        scatter(1, second_row)
-        nc.sync.dma_start(out[0, P:, segs[0]], second_row[:])
-        scatter(2, third_row)
-        nc.sync.dma_start(out[1, :P, segs[1]], third_row[:, segs[1]])
-        scatter(3, last_row)
-        nc.sync.dma_start(out[1, P:, segs[1]], last_row[:, segs[1]])
+        last_row = shared.tile([P, T], F32, name="last_row", offset=45 * KIB)
+        nc.gpsimd.memset(last_row[:, segs[1]], 0.0)
+        scatter(0, 1, scores[1], second_row)
+        scatter(1, 0, scores[2], third_row)
+        scatter(1, 1, scores[3], last_row)

@@ -34,7 +34,6 @@ def tile_attend_sddmm_kb_seg_kernel(tc, qT, k_words, k_scales, kb, offs, out):
         psum = ctx.enter_context(tc.psum_pool(name="psum", bufs=1))
 
         offsets = keep.tile([P, B * LIST_COLS], U16, name="offsets")
-        nc.sync.dma_start(offsets[:], offs)
         entries = [offsets[:, b * LIST_COLS : (b + 1) * LIST_COLS] for b in range(B)]
         segs = [slice(b * SEG, (b + 1) * SEG) for b in range(B)]
         slots = [slice(b * N, (b + 1) * N) for b in range(B)]
@@ -46,6 +45,7 @@ def tile_attend_sddmm_kb_seg_kernel(tc, qT, k_words, k_scales, kb, offs, out):
             pool_scales[P - held :, SEG:].bitcast(I32),
             k_scales[0].rearrange("f (b t) -> (f b) t", b=B).bitcast(I32),
         )
+        nc.sync.dma_start(offsets[:], offs)
         nc.vector.memset(pool_scales[: P - held, SEG:].bitcast(I32), 0)
 
         bias_down = []

@@ -6,6 +6,8 @@ B, N, T, D, NQ = 2, 512, 2048, 512, 256
 P = 128
 PACK = 4
 SEG = T // B
+HALF = N // 2
+LEAD = 128
 LIST_COLS = N // 16
 SCALE_ROWS = D // 32
 FLOPS = 2 * B * NQ * N * D
@@ -17,13 +19,11 @@ U32 = mybir.dt.uint32
 U16 = mybir.dt.uint16
 U8 = mybir.dt.uint8
 FP8X4 = mybir.dt.float8_e4m3fn_x4
-IDENTITY = mybir.ActivationFunctionType.Identity
+COPY = mybir.ActivationFunctionType.Copy
 ADD = mybir.AluOpType.add
 
 KIB = 1024
 BANK = 2 * KIB
-PER_PARTITION = SEG // P
-RAW_AT = (16 * KIB, 56 * KIB)
 
 
 def tile_attend_sddmm_kb_seg_kernel(tc, qT, k_words, k_scales, kb, offs, out):
@@ -33,13 +33,25 @@ def tile_attend_sddmm_kb_seg_kernel(tc, qT, k_words, k_scales, kb, offs, out):
         shared = ctx.enter_context(tc.tile_pool(name="shared", bufs=1))
         psum = ctx.enter_context(tc.psum_pool(name="psum", bufs=1))
 
+        def placed(name, shape, dtype, kib):
+            return shared.tile(shape, dtype, name=name, offset=int(kib * KIB), align_bytes=64)
+
         offsets = keep.tile([P, B * LIST_COLS], U16, name="offsets")
         entries = [offsets[:, b * LIST_COLS : (b + 1) * LIST_COLS] for b in range(B)]
+        halves = [slice(h * HALF, (h + 1) * HALF) for h in range(2)]
         segs = [slice(b * SEG, (b + 1) * SEG) for b in range(B)]
-        slots = [slice(b * N, (b + 1) * N) for b in range(B)]
         all_words = k_words[0].rearrange("p n t -> p (n t)").bitcast(I32)
 
-        pool_scales = keep.tile([P, T], U8, name="pool_scales", align_bytes=64)
+        def half_entries(b, h):
+            first = b * LIST_COLS + h * LIST_COLS // 2
+            return offsets[:, first : first + LIST_COLS // 2]
+
+        one = keep.tile([P, 8], F32, name="one")
+        nc.gpsimd.memset(one[:], 1.0)
+        ones = keep.tile([P, P], F32, name="ones")
+        nc.scalar.activation(ones[:], one[:, 0:1].to_broadcast([P, P]), COPY)
+
+        pool_scales = placed("pool_scales", [P, T], U8, 0)
         held = B * SCALE_ROWS
         nc.sync.dma_start(
             pool_scales[P - held :, SEG:].bitcast(I32),
@@ -48,140 +60,169 @@ def tile_attend_sddmm_kb_seg_kernel(tc, qT, k_words, k_scales, kb, offs, out):
         nc.sync.dma_start(offsets[:], offs)
         nc.vector.memset(pool_scales[: P - held, SEG:].bitcast(I32), 0)
 
-        bias_down = []
-        for b in range(B):
-            down = shared.tile([P, PER_PARTITION], F32, name=f"bias_down{b}", offset=(38 + 2 * b) * KIB)
-            nc.sync.dma_start(down[:], kb[0, segs[b]].rearrange("(p c) -> p c", p=P))
-            bias_down.append(down)
+        pool_bias = keep.tile([P, T], F32, name="pool_bias")
+        nc.sync.dma_start(pool_bias[P - B :, SEG:], kb[0].rearrange("(b t) -> b t", b=B))
+        nc.gpsimd.memset(pool_bias[: P - B, SEG:], 0.0)
 
-        pool_words, raw = [], []
+        raw0 = keep.tile([P, PACK, NQ], F32, name="raw0")
+        nc.sync.dma_start(raw0[:], qT[0].rearrange("(p j) w -> p j w", j=PACK))
+        pool_words = []
         for b in range(B):
             words = keep.tile([P, (b + 1) * SEG], U32, name=f"pool_words{b}")
             nc.sync.dma_start(words[:, segs[b]].bitcast(I32), all_words[:, segs[b]])
             pool_words.append(words)
-            rows = shared.tile([P, PACK, NQ], F32, name=f"q_raw{b}", offset=RAW_AT[b])
-            nc.sync.dma_start(rows[:], qT[b].rearrange("(p j) w -> p j w", j=PACK))
-            raw.append(rows)
 
         ident = keep.tile([P, P], F32, name="ident")
-        nc.gpsimd.memset(ident[:], 1.0)
         nc.gpsimd.affine_select(
             out=ident[:],
-            in_=ident[:],
+            in_=ones[:],
             compare_op=mybir.AluOpType.is_equal,
             fill=0.0,
             base=0,
             pattern=[[-1, P]],
             channel_multiplier=1,
         )
+        row00 = keep.tile([P, SEG], F32, name="row00")
+        nc.gpsimd.memset(row00[:], 0.0)
+        row01 = keep.tile([P, SEG], F32, name="row01")
+        nc.gpsimd.memset(row01[:], 0.0)
 
-        key_scales = []
-        for b in range(B):
-            plane = keep.tile([P, N], U8, name=f"key_scales{b}", align_bytes=64)
-            key_scales.append(plane)
-        first_row = keep.tile([P, SEG], F32, name="first_row")
-        nc.vector.memset(first_row[:].bitcast(I32), 0)
-
-        for b in range(B):
-            window = pool_scales[:, (1 - b) * SEG :]
+        def gather_scales(b):
             picked = keep.tile([P, N], U8, name=f"picked_scales{b}", align_bytes=64)
-            nc.vector.tensor_copy(picked[:], window.indirect(entries[b]))
+            nc.vector.tensor_copy(picked[:], pool_scales[:, (1 - b) * SEG :].indirect(entries[b]))
+            return picked
+
+        def move_scales(b, picked):
+            plane = keep.tile([P, N], U8, name=f"key_scales{b}", align_bytes=64)
             for r in range(4):
                 nc.sync.dma_start(
-                    key_scales[b][r:P:32, :].bitcast(I32),
+                    plane[r:P:32, :].bitcast(I32),
                     picked[P - held + B * r + b : P : 4 * B, :].bitcast(I32),
                 )
+            return plane
 
-        key_words = [
-            shared.tile([P, N], U32, name="key_words0", offset=44 * KIB, align_bytes=64),
-            shared.tile([P, N], U32, name="key_words1", offset=17 * KIB, align_bytes=64),
-        ]
-        nc.vector.tensor_copy(key_words[0][:], pool_words[0][:].indirect(entries[0]))
+        key_scales = [move_scales(0, gather_scales(0))]
+        picked1 = gather_scales(1)
+        raw1 = placed("raw1", [P, PACK, NQ], F32, 1)
+        nc.sync.dma_start(raw1[:], qT[1].rearrange("(p j) w -> p j w", j=PACK))
+        key_scales.append(move_scales(1, picked1))
 
-        def quantise(b, rounded):
-            nc.scalar.activation(
-                rounded[:].rearrange("p (c i) j -> p c j i", i=4),
-                raw[b][:].rearrange("p j (c i) -> p c j i", i=4),
-                IDENTITY,
+        def interleave(copy, rounded, raw):
+            copy(
+                rounded.rearrange("p (c i) j -> p c j i", i=4),
+                raw.rearrange("p j (c i) -> p c j i", i=4),
             )
-            q_words = keep.tile([P, NQ], U32, name=f"q_words{b}", align_bytes=64)
-            q_scales = keep.tile([P, NQ], U8, name=f"q_scales{b}", align_bytes=64)
+
+        def quantise(name, rounded, q_words):
+            q_scales = keep.tile([P, NQ], U8, name=f"q_scales{name}", align_bytes=64)
             nc.vector.quantize_mx(
                 out=q_words[:].bitcast(FP8X4),
                 scales=q_scales[:],
                 in_=rounded[:].rearrange("p w j -> p (w j)"),
             )
-            return q_words, q_scales
+            return [(q_words[:, j * P : (j + 1) * P], q_scales[:, j * P : (j + 1) * P]) for j in range(2)]
 
-        pool_bias = [
-            keep.tile([P, SEG], F32, name="pool_bias0"),
-            shared.tile([P, T], F32, name="pool_bias1", offset=19 * KIB + 512),
-        ]
-        groups = PER_PARTITION // 4
+        def gather_bias(b, picked):
+            nc.scalar.activation(picked[:], pool_bias[:, (1 - b) * SEG :].indirect(entries[b]), COPY)
 
-        def spread_bias(b):
-            by_group = pool_bias[b][:, segs[b]].rearrange("q (p g i) -> q g p i", g=groups, i=4)
-            for g in range(groups):
-                spread = psum.tile([P, 4, P], F32, name=f"spread{b}{g}", offset=(4 + groups * b + g) * BANK)
-                for i in range(4):
-                    c = 4 * g + i
-                    nc.tensor.transpose(spread[:, i, :], bias_down[b][:, c : c + 1].to_broadcast([P, P]), ident[:])
-                nc.scalar.copy(by_group[:, g], spread[:].rearrange("q i p -> q p i"))
+        def turn_bias(b, picked, bank):
+            turned = psum.tile([P, 4, P], F32, name=f"turned{b}", offset=bank * BANK)
+            for c in range(4):
+                nc.tensor.transpose(turned[:, c, :], picked[:, c * P : (c + 1) * P], ident[:])
+            return turned
 
-        spread_bias(0)
-        rounded0 = shared.tile([P, NQ, PACK], BF16, name="rounded0", offset=38 * KIB, align_bytes=64)
-        key_bias = keep.tile([P, B * N], F32, name="key_bias")
-        nc.vector.tensor_copy(key_bias[:, slots[0]], pool_bias[0][:].indirect(entries[0]))
-        queries = [quantise(0, rounded0)]
-        spread_bias(1)
-        nc.vector.tensor_copy(key_words[1][:], pool_words[1][:].indirect(entries[1]))
-        nc.vector.tensor_copy(key_bias[:, slots[1]], pool_bias[1][:].indirect(entries[1]))
+        def bias_columns(b, turned, columns):
+            nc.scalar.copy(columns[:], turned[:, :, P - B + b])
+            return columns
 
-        def product(b, j):
-            cols = slice(j * P, (j + 1) * P)
-            q_words, q_scales = queries[b]
-            bank = psum.tile([P, N], F32, name=f"bank{b}{j}", offset=(B * b + j) * BANK)
+        def spread_bias(b, columns, bank):
+            spread = psum.tile([P, 4, P], F32, name=f"spread{b}", offset=bank * BANK)
+            for c in range(4):
+                nc.tensor.transpose(spread[:, c, :], columns[:, c : c + 1].to_broadcast([P, P]), ident[:])
+            return spread
+
+        def keep_bias(b, spread, bias):
+            nc.scalar.copy(bias[:], spread[:].rearrange("q c p -> q (c p)"))
+            return bias
+
+        def product(name, bank, query, words, scales):
+            acc = psum.tile([P, words.shape[1]], F32, name=name, offset=bank * BANK)
             nc.tensor.matmul_mx(
-                out=bank[:],
-                lhsT=q_words[:, cols].bitcast(FP8X4),
-                lhsT_scale=q_scales[:, cols],
-                rhs=key_words[b][:].bitcast(FP8X4),
-                rhs_scale=key_scales[b][:],
+                out=acc[:],
+                lhsT=query[0].bitcast(FP8X4),
+                lhsT_scale=query[1],
+                rhs=words.bitcast(FP8X4),
+                rhs_scale=scales,
                 start=True,
                 stop=True,
             )
-            return bank
+            return acc
 
-        def scatter(b, j, score, row):
-            nc.vector.tensor_tensor(row[:].indirect(entries[b]), score[:], key_bias[:, slots[b]], ADD)
+        def store(b, j, row):
             nc.sync.dma_start(out[b, j * P : (j + 1) * P, segs[b]], row[:, segs[b]])
 
-        scores = [
-            keep.tile([P, N], F32, name="score0"),
-            shared.tile([P, N], F32, name="score1", offset=RAW_AT[1]),
-            keep.tile([P, N], F32, name="score2"),
-            keep.tile([P, N], F32, name="score3"),
-        ]
-        banks = [product(0, 0), product(0, 1)]
-        nc.scalar.copy(scores[0][:], banks[0][:])
-        second_row = shared.tile([P, SEG], F32, name="second_row", offset=20 * KIB)
-        nc.gpsimd.memset(second_row[:], 0.0)
-        zeros = shared.tile([P, SEG], F32, name="zeros", offset=24 * KIB)
+        picked_bias0 = placed("picked_bias0", [P, N], F32, 16)
+        gather_bias(0, picked_bias0)
+        turned0 = turn_bias(0, picked_bias0, 4)
+        zeros = placed("zeros", [P, SEG], F32, 16)
         nc.gpsimd.memset(zeros[:], 0.0)
-
-        scatter(0, 0, scores[0], first_row)
-        rounded1 = shared.tile([P, NQ, PACK], BF16, name="rounded1", offset=44 * KIB, align_bytes=64)
-        queries.append(quantise(1, rounded1))
-        nc.scalar.copy(scores[1][:], banks[1][:])
         for b in range(B):
             for j in range(NQ // P):
-                nc.scalar.dma_start(out[b, j * P : (j + 1) * P, segs[1 - b]], zeros[:])
-        for j in range(NQ // P):
-            nc.scalar.copy(scores[2 + j][:], product(1, j)[:])
-        third_row = shared.tile([P, T], F32, name="third_row", offset=37 * KIB)
-        nc.gpsimd.memset(third_row[:, segs[1]], 0.0)
-        last_row = shared.tile([P, T], F32, name="last_row", offset=45 * KIB)
-        nc.gpsimd.memset(last_row[:, segs[1]], 0.0)
-        scatter(0, 1, scores[1], second_row)
-        scatter(1, 0, scores[2], third_row)
-        scatter(1, 1, scores[3], last_row)
+                nc.sync.dma_start(out[b, j * P : (j + 1) * P, segs[1 - b]], zeros[:])
+        picked_bias1 = keep.tile([P, N], F32, name="picked_bias1")
+        gather_bias(1, picked_bias1)
+        turned1 = turn_bias(1, picked_bias1, 6)
+        rounded0 = placed("rounded0", [P, NQ, PACK], BF16, 44)
+        interleave(nc.scalar.copy, rounded0[:, :P, :], raw0[:, :, :P])
+        columns0 = bias_columns(0, turned0, placed("columns0", [P, 4], F32, 6))
+        interleave(nc.scalar.copy, rounded0[:, P:, :], raw0[:, :, P:])
+        columns1 = bias_columns(1, turned1, keep.tile([P, 4], F32, name="columns1"))
+        spread0 = spread_bias(0, columns0, 5)
+        spread1 = spread_bias(1, columns1, 7)
+        bias0 = keep_bias(0, spread0, keep.tile([P, N], F32, name="key_bias0"))
+        bias1 = keep_bias(1, spread1, keep.tile([P, N], F32, name="key_bias1"))
+
+        words0 = placed("words0", [P, N], U32, 37)
+        nc.vector.tensor_copy(words0[:], pool_words[0][:].indirect(entries[0]))
+        query0 = quantise("0", rounded0, placed("q_words0", [P, NQ], U32, 6))
+        acc0 = [product(f"acc0{j}", j, query0[j], words0[:], key_scales[0][:]) for j in range(2)]
+
+        words1 = placed("words1", [P, N], U32, 45)
+        nc.vector.tensor_copy(words1[:], pool_words[1][:].indirect(entries[1]))
+        score00a = keep.tile([P, LEAD], F32, name="score00a")
+        nc.vector.tensor_tensor(score00a[:], acc0[0][:, :LEAD], bias0[:, :LEAD], ADD)
+        nc.scalar.activation(row00[:].indirect(offsets[:, : LEAD // 16]), score00a[:], COPY)
+        score01b = keep.tile([P, HALF], F32, name="score01b")
+        nc.scalar.copy(score01b[:], acc0[1][:, halves[1]])
+
+        rounded1 = placed("rounded1", [P, NQ, PACK], BF16, 36.5)
+        interleave(nc.vector.tensor_copy, rounded1[:], raw1[:])
+        query1 = quantise("1", rounded1, keep.tile([P, NQ], U32, name="q_words1", align_bytes=64))
+        acc10 = [product(f"acc10{h}", 2 + h, query1[0], words1[:, halves[h]], key_scales[1][:, halves[h]]) for h in range(2)]
+        acc11 = product("acc11", 4, query1[1], words1[:], key_scales[1][:])
+
+        score01 = [placed("score01a", [P, HALF], F32, 36.75), score01b]
+        nc.scalar.copy(score01[0][:], acc0[1][:, halves[0]])
+        score00b = placed("score00b", [P, N - LEAD], F32, 37.75)
+        nc.vector.tensor_tensor(score00b[:], acc0[0][:, LEAD:], bias0[:, LEAD:], ADD)
+        nc.scalar.activation(row00[:].indirect(offsets[:, LEAD // 16 : LIST_COLS]), score00b[:], COPY)
+        store(0, 0, row00)
+        row10 = placed("row10", [P, T], F32, 28.75)
+        nc.gpsimd.memset(row10[:, segs[1]], 0.0)
+        row11 = placed("row11", [P, T], F32, 46.5)
+        nc.gpsimd.memset(row11[:, segs[1]], 0.0)
+
+        nc.vector.tensor_tensor(row01[:].indirect(half_entries(0, 0)), score01[0][:], bias0[:, halves[0]], ADD)
+        score10 = [placed("score10a", [P, HALF], F32, 36.75), keep.tile([P, HALF], F32, name="score10b")]
+        for h in range(2):
+            nc.vector.tensor_tensor(score10[h][:], acc10[h][:], bias1[:, halves[h]], ADD)
+        nc.vector.tensor_tensor(row01[:].indirect(half_entries(0, 1)), score01[1][:], bias0[:, halves[1]], ADD)
+        store(0, 1, row01)
+
+        score11 = placed("score11", [P, N], F32, 38.5)
+        nc.scalar.copy(score11[:], acc11[:])
+        for h in range(2):
+            nc.scalar.activation(row10[:].indirect(half_entries(1, h)), score10[h][:], COPY)
+        store(1, 0, row10)
+        nc.vector.tensor_tensor(row11[:].indirect(entries[1]), score11[:], bias1[:], ADD)
+        store(1, 1, row11)

@@ -192,34 +192,32 @@ def tile_attend_sddmm_kb_seg_kernel(tc, qT, k_words, k_scales, kb, offs, out):
         score00a = keep.tile([P, LEAD], F32, name="score00a")
         nc.vector.tensor_tensor(score00a[:], acc0[0][:, :LEAD], bias0[:, :LEAD], ADD)
         nc.scalar.activation(row00[:].indirect(offsets[:, : LEAD // 16]), score00a[:], COPY)
-        score01b = keep.tile([P, HALF], F32, name="score01b")
-        nc.scalar.copy(score01b[:], acc0[1][:, halves[1]])
 
-        rounded1 = placed("rounded1", [P, NQ, PACK], BF16, 36.5)
+        rounded1 = placed("rounded1", [P, NQ, PACK], BF16, 36.25)
         interleave(nc.vector.tensor_copy, rounded1[:], raw1[:])
         query1 = quantise("1", rounded1, keep.tile([P, NQ], U32, name="q_words1", align_bytes=64))
         acc10 = [product(f"acc10{h}", 2 + h, query1[0], words1[:, halves[h]], key_scales[1][:, halves[h]]) for h in range(2)]
         acc11 = product("acc11", 4, query1[1], words1[:], key_scales[1][:])
 
-        score01 = [placed("score01a", [P, HALF], F32, 36.75), score01b]
-        nc.scalar.copy(score01[0][:], acc0[1][:, halves[0]])
-        score00b = placed("score00b", [P, N - LEAD], F32, 37.75)
+        score01 = placed("score01", [P, N], F32, 38)
+        nc.scalar.copy(score01[:], acc0[1][:])
+        score00b = placed("score00b", [P, N - LEAD], F32, 36.5)
         nc.vector.tensor_tensor(score00b[:], acc0[0][:, LEAD:], bias0[:, LEAD:], ADD)
         nc.scalar.activation(row00[:].indirect(offsets[:, LEAD // 16 : LIST_COLS]), score00b[:], COPY)
         store(0, 0, row00)
-        row10 = placed("row10", [P, T], F32, 28.75)
-        nc.gpsimd.memset(row10[:, segs[1]], 0.0)
-        row11 = placed("row11", [P, T], F32, 46.5)
+        row11 = placed("row11", [P, T], F32, 28.5)
         nc.gpsimd.memset(row11[:, segs[1]], 0.0)
+        row10 = placed("row10", [P, T], F32, 46.5)
+        nc.gpsimd.memset(row10[:, segs[1]], 0.0)
 
-        nc.vector.tensor_tensor(row01[:].indirect(half_entries(0, 0)), score01[0][:], bias0[:, halves[0]], ADD)
-        score10 = [placed("score10a", [P, HALF], F32, 36.75), keep.tile([P, HALF], F32, name="score10b")]
+        score10 = []
         for h in range(2):
+            score10.append(keep.tile([P, HALF], F32, name=f"score10{h}"))
             nc.vector.tensor_tensor(score10[h][:], acc10[h][:], bias1[:, halves[h]], ADD)
-        nc.vector.tensor_tensor(row01[:].indirect(half_entries(0, 1)), score01[1][:], bias0[:, halves[1]], ADD)
+        nc.vector.tensor_tensor(row01[:].indirect(entries[0]), score01[:], bias0[:], ADD)
         store(0, 1, row01)
 
-        score11 = placed("score11", [P, N], F32, 38.5)
+        score11 = keep.tile([P, N], F32, name="score11")
         nc.scalar.copy(score11[:], acc11[:])
         for h in range(2):
             nc.scalar.activation(row10[:].indirect(half_entries(1, h)), score10[h][:], COPY)

@@ -7,7 +7,7 @@ P = 128
 PACK = 4
 SEG = T // B
 HALF = N // 2
-LEAD = 128
+ZERO_COLS = SEG // 2
 LIST_COLS = N // 16
 SCALE_ROWS = D // 32
 FLOPS = 2 * B * NQ * N * D
@@ -51,14 +51,10 @@ def tile_attend_sddmm_kb_seg_kernel(tc, qT, k_words, k_scales, kb, offs, out):
         ones = keep.tile([P, P], F32, name="ones")
         nc.scalar.activation(ones[:], one[:, 0:1].to_broadcast([P, P]), COPY)
 
-        pool_scales = placed("pool_scales", [P, T], U8, 0)
-        held = B * SCALE_ROWS
-        nc.sync.dma_start(
-            pool_scales[P - held :, SEG:].bitcast(I32),
-            k_scales[0].rearrange("f (b t) -> (f b) t", b=B).bitcast(I32),
-        )
+        pool_scales = keep.tile([P, T], U8, name="pool_scales", align_bytes=64)
+        nc.sync.dma_start(pool_scales[P - SCALE_ROWS :, :].bitcast(I32), k_scales[0].bitcast(I32))
         nc.sync.dma_start(offsets[:], offs)
-        nc.vector.memset(pool_scales[: P - held, SEG:].bitcast(I32), 0)
+        nc.vector.memset(pool_scales[: P - SCALE_ROWS, :].bitcast(I32), 0)
 
         pool_bias = keep.tile([P, T], F32, name="pool_bias")
         nc.sync.dma_start(pool_bias[P - B :, SEG:], kb[0].rearrange("(b t) -> b t", b=B))
@@ -71,7 +67,11 @@ def tile_attend_sddmm_kb_seg_kernel(tc, qT, k_words, k_scales, kb, offs, out):
             words = keep.tile([P, (b + 1) * SEG], U32, name=f"pool_words{b}")
             nc.sync.dma_start(words[:, segs[b]].bitcast(I32), all_words[:, segs[b]])
             pool_words.append(words)
+        raw1 = keep.tile([P, PACK, NQ], F32, name="raw1")
+        nc.sync.dma_start(raw1[:], qT[1].rearrange("(p j) w -> p j w", j=PACK))
 
+        row00 = keep.tile([P, SEG], F32, name="row00")
+        nc.gpsimd.memset(row00[:], 0.0)
         ident = keep.tile([P, P], F32, name="ident")
         nc.gpsimd.affine_select(
             out=ident[:],
@@ -82,30 +82,16 @@ def tile_attend_sddmm_kb_seg_kernel(tc, qT, k_words, k_scales, kb, offs, out):
             pattern=[[-1, P]],
             channel_multiplier=1,
         )
-        row00 = keep.tile([P, SEG], F32, name="row00")
-        nc.gpsimd.memset(row00[:], 0.0)
-        row01 = keep.tile([P, SEG], F32, name="row01")
-        nc.gpsimd.memset(row01[:], 0.0)
 
-        def gather_scales(b):
-            picked = keep.tile([P, N], U8, name=f"picked_scales{b}", align_bytes=64)
-            nc.vector.tensor_copy(picked[:], pool_scales[:, (1 - b) * SEG :].indirect(entries[b]))
-            return picked
-
-        def move_scales(b, picked):
-            plane = keep.tile([P, N], U8, name=f"key_scales{b}", align_bytes=64)
-            for r in range(4):
-                nc.sync.dma_start(
-                    plane[r:P:32, :].bitcast(I32),
-                    picked[P - held + B * r + b : P : 4 * B, :].bitcast(I32),
-                )
-            return plane
-
-        key_scales = [move_scales(0, gather_scales(0))]
-        picked1 = gather_scales(1)
-        raw1 = placed("raw1", [P, PACK, NQ], F32, 1)
-        nc.sync.dma_start(raw1[:], qT[1].rearrange("(p j) w -> p j w", j=PACK))
-        key_scales.append(move_scales(1, picked1))
+        picked_scales = keep.tile([P, B * N], U8, name="picked_scales", align_bytes=64)
+        nc.vector.tensor_copy(picked_scales[:], pool_scales[:].indirect(offsets[:]))
+        planes = keep.tile([P, B * N], U8, name="planes", align_bytes=64)
+        for r in range(4):
+            nc.sync.dma_start(
+                planes[r:P:32, :].bitcast(I32),
+                picked_scales[P - SCALE_ROWS + r : P : 4, :].bitcast(I32),
+            )
+        key_scales = [planes[:, b * N : (b + 1) * N] for b in range(B)]
 
         def interleave(copy, rounded, raw):
             copy(
@@ -132,7 +118,7 @@ def tile_attend_sddmm_kb_seg_kernel(tc, qT, k_words, k_scales, kb, offs, out):
             return turned
 
         def bias_columns(b, turned, columns):
-            nc.scalar.copy(columns[:], turned[:, :, P - B + b])
+            nc.scalar.copy(columns, turned[:, :, P - B + b])
             return columns
 
         def spread_bias(b, columns, bank):
@@ -161,66 +147,61 @@ def tile_attend_sddmm_kb_seg_kernel(tc, qT, k_words, k_scales, kb, offs, out):
         def store(b, j, row):
             nc.sync.dma_start(out[b, j * P : (j + 1) * P, segs[b]], row[:, segs[b]])
 
-        picked_bias0 = placed("picked_bias0", [P, N], F32, 16)
-        gather_bias(0, picked_bias0)
-        turned0 = turn_bias(0, picked_bias0, 4)
-        zeros = placed("zeros", [P, SEG], F32, 16)
-        nc.gpsimd.memset(zeros[:], 0.0)
+        picked_bias = [keep.tile([P, N], F32, name="picked_bias0"), placed("picked_bias1", [P, N], F32, 0)]
+        turned = []
+        for b in range(B):
+            gather_bias(b, picked_bias[b])
+            turned.append(turn_bias(b, picked_bias[b], 4 + b))
+        rounded0 = keep.tile([P, NQ, PACK], BF16, name="rounded0", align_bytes=64)
+        interleave(nc.scalar.copy, rounded0[:], raw0[:])
+        columns0 = bias_columns(0, turned[0], shared.tile([P, 16], F32, name="columns0", offset=4 * KIB - 32)[:, :4])
+        columns1 = bias_columns(1, turned[1], keep.tile([P, 4], F32, name="columns1")[:])
+        zeros = placed("zeros", [P, ZERO_COLS], F32, 0)
+        nc.scalar.activation(zeros[:], ones[:, 0:1].to_broadcast([P, ZERO_COLS]), COPY, scale=0.0)
         for b in range(B):
             for j in range(NQ // P):
-                nc.sync.dma_start(out[b, j * P : (j + 1) * P, segs[1 - b]], zeros[:])
-        picked_bias1 = keep.tile([P, N], F32, name="picked_bias1")
-        gather_bias(1, picked_bias1)
-        turned1 = turn_bias(1, picked_bias1, 6)
-        rounded0 = placed("rounded0", [P, NQ, PACK], BF16, 44)
-        interleave(nc.scalar.copy, rounded0[:, :P, :], raw0[:, :, :P])
-        columns0 = bias_columns(0, turned0, placed("columns0", [P, 4], F32, 6))
-        interleave(nc.scalar.copy, rounded0[:, P:, :], raw0[:, :, P:])
-        columns1 = bias_columns(1, turned1, keep.tile([P, 4], F32, name="columns1"))
-        spread0 = spread_bias(0, columns0, 5)
-        spread1 = spread_bias(1, columns1, 7)
-        bias0 = keep_bias(0, spread0, keep.tile([P, N], F32, name="key_bias0"))
-        bias1 = keep_bias(1, spread1, keep.tile([P, N], F32, name="key_bias1"))
+                nc.sync.dma_start(
+                    out[b, j * P : (j + 1) * P, segs[1 - b]].rearrange("p (r c) -> p r c", c=ZERO_COLS),
+                    zeros[:].unsqueeze(1).to_broadcast([P, SEG // ZERO_COLS, ZERO_COLS]),
+                )
+        spread = [spread_bias(b, columns, 6 + b) for b, columns in enumerate((columns0, columns1))]
 
-        words0 = placed("words0", [P, N], U32, 37)
-        nc.vector.tensor_copy(words0[:], pool_words[0][:].indirect(entries[0]))
-        query0 = quantise("0", rounded0, placed("q_words0", [P, NQ], U32, 6))
-        acc0 = [product(f"acc0{j}", j, query0[j], words0[:], key_scales[0][:]) for j in range(2)]
-
-        words1 = placed("words1", [P, N], U32, 45)
-        nc.vector.tensor_copy(words1[:], pool_words[1][:].indirect(entries[1]))
-        score00a = keep.tile([P, LEAD], F32, name="score00a")
-        nc.vector.tensor_tensor(score00a[:], acc0[0][:, :LEAD], bias0[:, :LEAD], ADD)
-        nc.scalar.activation(row00[:].indirect(offsets[:, : LEAD // 16]), score00a[:], COPY)
-
-        rounded1 = placed("rounded1", [P, NQ, PACK], BF16, 36.25)
-        interleave(nc.vector.tensor_copy, rounded1[:], raw1[:])
-        query1 = quantise("1", rounded1, keep.tile([P, NQ], U32, name="q_words1", align_bytes=64))
-        acc10 = [product(f"acc10{h}", 2 + h, query1[0], words1[:, halves[h]], key_scales[1][:, halves[h]]) for h in range(2)]
-        acc11 = product("acc11", 4, query1[1], words1[:], key_scales[1][:])
-
-        score01 = placed("score01", [P, N], F32, 38)
-        nc.scalar.copy(score01[:], acc0[1][:])
-        score00b = placed("score00b", [P, N - LEAD], F32, 36.5)
-        nc.vector.tensor_tensor(score00b[:], acc0[0][:, LEAD:], bias0[:, LEAD:], ADD)
-        nc.scalar.activation(row00[:].indirect(offsets[:, LEAD // 16 : LIST_COLS]), score00b[:], COPY)
-        store(0, 0, row00)
-        row11 = placed("row11", [P, T], F32, 28.5)
-        nc.gpsimd.memset(row11[:, segs[1]], 0.0)
-        row10 = placed("row10", [P, T], F32, 46.5)
+        words = [keep.tile([P, N], U32, name="words0", align_bytes=64), placed("words1", [P, N], U32, 16)]
+        for b in range(B):
+            nc.vector.tensor_copy(words[b][:], pool_words[b][:].indirect(entries[b]))
+        query0 = quantise("0", rounded0, placed("q_words0", [P, NQ], U32, 3))
+        rounded1 = placed("rounded1", [P, NQ, PACK], BF16, 4)
+        interleave(nc.scalar.copy, rounded1[:], raw1[:])
+        query1 = quantise("1", rounded1, placed("q_words1", [P, NQ], U32, 24))
+        acc = {}
+        for b, query in enumerate((query0, query1)):
+            for j in range(2):
+                acc[b, j] = product(f"acc{b}{j}", B * b + j, query[j], words[b][:], key_scales[b])
+        bias0 = keep_bias(0, spread[0], keep.tile([P, N], F32, name="key_bias0"))
+        bias1 = keep_bias(1, spread[1], keep.tile([P, N], F32, name="key_bias1"))
+        row10 = placed("row10", [P, T], F32, 5.5)
         nc.gpsimd.memset(row10[:, segs[1]], 0.0)
 
-        score10 = []
         for h in range(2):
-            score10.append(keep.tile([P, HALF], F32, name=f"score10{h}"))
-            nc.vector.tensor_tensor(score10[h][:], acc10[h][:], bias1[:, halves[h]], ADD)
-        nc.vector.tensor_tensor(row01[:].indirect(entries[0]), score01[:], bias0[:], ADD)
-        store(0, 1, row01)
+            score = keep.tile([P, HALF], F32, name=f"score00{h}")
+            nc.vector.tensor_tensor(score[:], acc[0, 0][:, halves[h]], bias0[:, halves[h]], ADD)
+            nc.scalar.activation(row00[:].indirect(half_entries(0, h)), score[:], COPY)
+        store(0, 0, row00)
+        score01 = keep.tile([P, N], F32, name="score01")
+        nc.vector.tensor_tensor(score01[:], acc[0, 1][:], bias0[:], ADD)
+        score10 = keep.tile([P, N], F32, name="score10")
+        nc.vector.tensor_copy(score10[:], acc[1, 0][:])
+        nc.vector.tensor_tensor(row10[:].indirect(entries[1]), score10[:], bias1[:], ADD)
+        store(1, 0, row10)
 
         score11 = keep.tile([P, N], F32, name="score11")
-        nc.scalar.copy(score11[:], acc11[:])
+        nc.scalar.copy(score11[:], acc[1, 1][:])
+        row01 = placed("row01", [P, SEG], F32, 17)
+        nc.gpsimd.memset(row01[:], 0.0)
+        row11 = placed("row11", [P, T], F32, 24)
+        nc.gpsimd.memset(row11[:, segs[1]], 0.0)
         for h in range(2):
-            nc.scalar.activation(row10[:].indirect(half_entries(1, h)), score10[h][:], COPY)
-        store(1, 0, row10)
+            nc.scalar.activation(row01[:].indirect(half_entries(0, h)), score01[:, halves[h]], COPY)
+        store(0, 1, row01)
         nc.vector.tensor_tensor(row11[:].indirect(entries[1]), score11[:], bias1[:], ADD)
         store(1, 1, row11)

@@ -21,6 +21,7 @@ U8 = mybir.dt.uint8
 FP8X4 = mybir.dt.float8_e4m3fn_x4
 COPY = mybir.ActivationFunctionType.Copy
 ADD = mybir.AluOpType.add
+MULT = mybir.AluOpType.mult
 
 KIB = 1024
 BANK = 2 * KIB
@@ -60,15 +61,12 @@ def tile_attend_sddmm_kb_seg_kernel(tc, qT, k_words, k_scales, kb, offs, out):
         nc.sync.dma_start(pool_bias[P - B :, SEG:], kb[0].rearrange("(b t) -> b t", b=B))
         nc.gpsimd.memset(pool_bias[: P - B, SEG:], 0.0)
 
-        raw0 = keep.tile([P, PACK, NQ], F32, name="raw0")
-        nc.sync.dma_start(raw0[:], qT[0].rearrange("(p j) w -> p j w", j=PACK))
-        pool_words = []
+        raws, pool_words = [], []
         for b in range(B):
-            words = keep.tile([P, (b + 1) * SEG], U32, name=f"pool_words{b}")
-            nc.sync.dma_start(words[:, segs[b]].bitcast(I32), all_words[:, segs[b]])
-            pool_words.append(words)
-        raw1 = keep.tile([P, PACK, NQ], F32, name="raw1")
-        nc.sync.dma_start(raw1[:], qT[1].rearrange("(p j) w -> p j w", j=PACK))
+            raws.append(keep.tile([P, PACK, NQ], F32, name=f"raw{b}"))
+            nc.sync.dma_start(raws[b][:], qT[b].rearrange("(p j) w -> p j w", j=PACK))
+            pool_words.append(keep.tile([P, (b + 1) * SEG], U32, name=f"pool_words{b}"))
+            nc.sync.dma_start(pool_words[b][:, segs[b]].bitcast(I32), all_words[:, segs[b]])
 
         row00 = keep.tile([P, SEG], F32, name="row00")
         nc.gpsimd.memset(row00[:], 0.0)
@@ -93,11 +91,8 @@ def tile_attend_sddmm_kb_seg_kernel(tc, qT, k_words, k_scales, kb, offs, out):
             )
         key_scales = [planes[:, b * N : (b + 1) * N] for b in range(B)]
 
-        def interleave(copy, rounded, raw):
-            copy(
-                rounded.rearrange("p (c i) j -> p c j i", i=4),
-                raw.rearrange("p j (c i) -> p c j i", i=4),
-            )
+        def round_queries(rounded, raw):
+            nc.gpsimd.tensor_scalar(rounded[:], raw[:].rearrange("p j w -> p w j"), 1.0, 0.0, MULT, ADD)
 
         def quantise(name, rounded, q_words):
             q_scales = keep.tile([P, NQ], U8, name=f"q_scales{name}", align_bytes=64)
@@ -147,15 +142,17 @@ def tile_attend_sddmm_kb_seg_kernel(tc, qT, k_words, k_scales, kb, offs, out):
         def store(b, j, row):
             nc.sync.dma_start(out[b, j * P : (j + 1) * P, segs[b]], row[:, segs[b]])
 
-        picked_bias = [keep.tile([P, N], F32, name="picked_bias0"), placed("picked_bias1", [P, N], F32, 0)]
+        rounded = []
+        for b, raw in enumerate(raws):
+            rounded.append(placed(f"rounded{b}", [P, NQ, PACK], BF16, 40 - 36 * b))
+            round_queries(rounded[b], raw)
+
+        picked_bias = [placed("picked_bias0", [P, N], F32, 0), keep.tile([P, N], F32, name="picked_bias1")]
         turned = []
         for b in range(B):
             gather_bias(b, picked_bias[b])
             turned.append(turn_bias(b, picked_bias[b], 4 + b))
-        rounded0 = keep.tile([P, NQ, PACK], BF16, name="rounded0", align_bytes=64)
-        interleave(nc.scalar.copy, rounded0[:], raw0[:])
-        columns0 = bias_columns(0, turned[0], shared.tile([P, 16], F32, name="columns0", offset=4 * KIB - 32)[:, :4])
-        columns1 = bias_columns(1, turned[1], keep.tile([P, 4], F32, name="columns1")[:])
+        columns = [bias_columns(0, turned[0], keep.tile([P, 4], F32, name="columns0")[:])]
         zeros = placed("zeros", [P, ZERO_COLS], F32, 0)
         nc.scalar.activation(zeros[:], ones[:, 0:1].to_broadcast([P, ZERO_COLS]), COPY, scale=0.0)
         for b in range(B):
@@ -164,21 +161,20 @@ def tile_attend_sddmm_kb_seg_kernel(tc, qT, k_words, k_scales, kb, offs, out):
                     out[b, j * P : (j + 1) * P, segs[1 - b]].rearrange("p (r c) -> p r c", c=ZERO_COLS),
                     zeros[:].unsqueeze(1).to_broadcast([P, SEG // ZERO_COLS, ZERO_COLS]),
                 )
-        spread = [spread_bias(b, columns, 6 + b) for b, columns in enumerate((columns0, columns1))]
+        columns.append(bias_columns(1, turned[1], keep.tile([P, 4], F32, name="columns1")[:]))
+        spread = [spread_bias(b, columns[b], 6 + b) for b in range(B)]
+        bias0 = keep_bias(0, spread[0], keep.tile([P, N], F32, name="key_bias0"))
+        bias1 = keep_bias(1, spread[1], keep.tile([P, N], F32, name="key_bias1"))
 
-        words = [keep.tile([P, N], U32, name="words0", align_bytes=64), placed("words1", [P, N], U32, 16)]
+        query0 = quantise("0", rounded[0], keep.tile([P, NQ], U32, name="q_words0", align_bytes=64))
+        words = [keep.tile([P, N], U32, name="words0", align_bytes=64), placed("words1", [P, N], U32, 41)]
         for b in range(B):
             nc.vector.tensor_copy(words[b][:], pool_words[b][:].indirect(entries[b]))
-        query0 = quantise("0", rounded0, placed("q_words0", [P, NQ], U32, 3))
-        rounded1 = placed("rounded1", [P, NQ, PACK], BF16, 4)
-        interleave(nc.scalar.copy, rounded1[:], raw1[:])
-        query1 = quantise("1", rounded1, placed("q_words1", [P, NQ], U32, 24))
+        query1 = quantise("1", rounded[1], placed("q_words1", [P, NQ], U32, 24))
         acc = {}
         for b, query in enumerate((query0, query1)):
             for j in range(2):
                 acc[b, j] = product(f"acc{b}{j}", B * b + j, query[j], words[b][:], key_scales[b])
-        bias0 = keep_bias(0, spread[0], keep.tile([P, N], F32, name="key_bias0"))
-        bias1 = keep_bias(1, spread[1], keep.tile([P, N], F32, name="key_bias1"))
         row10 = placed("row10", [P, T], F32, 5.5)
         nc.gpsimd.memset(row10[:, segs[1]], 0.0)
 
@@ -196,7 +192,7 @@ def tile_attend_sddmm_kb_seg_kernel(tc, qT, k_words, k_scales, kb, offs, out):
 
         score11 = keep.tile([P, N], F32, name="score11")
         nc.scalar.copy(score11[:], acc[1, 1][:])
-        row01 = placed("row01", [P, SEG], F32, 17)
+        row01 = placed("row01", [P, SEG], F32, 42.5)
         nc.gpsimd.memset(row01[:], 0.0)
         row11 = placed("row11", [P, T], F32, 24)
         nc.gpsimd.memset(row11[:, segs[1]], 0.0)

@@ -63,7 +63,7 @@ def tile_attend_sddmm_kb_seg_kernel(tc, qT, k_words, k_scales, kb, offs, out):
 
         raws, pool_words = [], []
         for b in range(B):
-            raws.append(keep.tile([P, PACK, NQ], F32, name=f"raw{b}"))
+            raws.append(placed(f"raw{b}", [P, PACK, NQ], F32, 48 + 4 * b))
             nc.sync.dma_start(raws[b][:], qT[b].rearrange("(p j) w -> p j w", j=PACK))
             pool_words.append(keep.tile([P, (b + 1) * SEG], U32, name=f"pool_words{b}"))
             nc.sync.dma_start(pool_words[b][:, segs[b]].bitcast(I32), all_words[:, segs[b]])
@@ -147,34 +147,38 @@ def tile_attend_sddmm_kb_seg_kernel(tc, qT, k_words, k_scales, kb, offs, out):
             rounded.append(placed(f"rounded{b}", [P, NQ, PACK], BF16, 40 - 36 * b))
             round_queries(rounded[b], raw)
 
-        picked_bias = [placed("picked_bias0", [P, N], F32, 0), keep.tile([P, N], F32, name="picked_bias1")]
+        picked_bias = [keep.tile([P, N], F32, name="picked_bias0"), keep.tile([P, N], F32, name="picked_bias1")]
         turned = []
         for b in range(B):
             gather_bias(b, picked_bias[b])
             turned.append(turn_bias(b, picked_bias[b], 4 + b))
         columns = [bias_columns(0, turned[0], keep.tile([P, 4], F32, name="columns0")[:])]
-        zeros = placed("zeros", [P, ZERO_COLS], F32, 0)
-        nc.scalar.activation(zeros[:], ones[:, 0:1].to_broadcast([P, ZERO_COLS]), COPY, scale=0.0)
-        for b in range(B):
-            for j in range(NQ // P):
-                nc.sync.dma_start(
-                    out[b, j * P : (j + 1) * P, segs[1 - b]].rearrange("p (r c) -> p r c", c=ZERO_COLS),
-                    zeros[:].unsqueeze(1).to_broadcast([P, SEG // ZERO_COLS, ZERO_COLS]),
-                )
         columns.append(bias_columns(1, turned[1], keep.tile([P, 4], F32, name="columns1")[:]))
         spread = [spread_bias(b, columns[b], 6 + b) for b in range(B)]
         bias0 = keep_bias(0, spread[0], keep.tile([P, N], F32, name="key_bias0"))
         bias1 = keep_bias(1, spread[1], keep.tile([P, N], F32, name="key_bias1"))
 
         query0 = quantise("0", rounded[0], keep.tile([P, NQ], U32, name="q_words0", align_bytes=64))
-        words = [keep.tile([P, N], U32, name="words0", align_bytes=64), placed("words1", [P, N], U32, 41)]
+        zeros = placed("zeros", [P, ZERO_COLS], F32, 48)
+        nc.vector.memset(zeros[:], 0.0)
+        for b in range(B):
+            for j in range(NQ // P):
+                nc.sync.dma_start(
+                    out[b, j * P : (j + 1) * P, segs[1 - b]].rearrange("p (r c) -> p r c", c=ZERO_COLS),
+                    zeros[:].unsqueeze(1).to_broadcast([P, SEG // ZERO_COLS, ZERO_COLS]),
+                )
+        words = [placed("words0", [P, N], U32, 39), placed("words1", [P, N], U32, 41)]
         for b in range(B):
             nc.vector.tensor_copy(words[b][:], pool_words[b][:].indirect(entries[b]))
         query1 = quantise("1", rounded[1], placed("q_words1", [P, NQ], U32, 24))
         acc = {}
-        for b, query in enumerate((query0, query1)):
-            for j in range(2):
-                acc[b, j] = product(f"acc{b}{j}", B * b + j, query[j], words[b][:], key_scales[b])
+        for j in range(2):
+            acc[0, j] = product(f"acc0{j}", j, query0[j], words[0][:], key_scales[0])
+        acc[1, 0] = product("acc10", 2, query1[0], words[1][:], key_scales[1])
+        last = [
+            product(f"acc11{h}", 3 + h, query1[1], words[1][:, halves[h]], key_scales[1][:, halves[h]])
+            for h in range(2)
+        ]
         row10 = placed("row10", [P, T], F32, 5.5)
         nc.gpsimd.memset(row10[:, segs[1]], 0.0)
 
@@ -187,11 +191,12 @@ def tile_attend_sddmm_kb_seg_kernel(tc, qT, k_words, k_scales, kb, offs, out):
         nc.vector.tensor_tensor(score01[:], acc[0, 1][:], bias0[:], ADD)
         score10 = keep.tile([P, N], F32, name="score10")
         nc.vector.tensor_copy(score10[:], acc[1, 0][:])
+        score11 = keep.tile([P, N], F32, name="score11")
+        nc.vector.tensor_copy(score11[:, halves[0]], last[0][:])
         nc.vector.tensor_tensor(row10[:].indirect(entries[1]), score10[:], bias1[:], ADD)
         store(1, 0, row10)
 
-        score11 = keep.tile([P, N], F32, name="score11")
-        nc.scalar.copy(score11[:], acc[1, 1][:])
+        nc.scalar.copy(score11[:, halves[1]], last[1][:])
         row01 = placed("row01", [P, SEG], F32, 42.5)
         nc.gpsimd.memset(row01[:], 0.0)
         row11 = placed("row11", [P, T], F32, 24)

@@ -49,17 +49,18 @@ def tile_attend_sddmm_kb_seg_kernel(tc, qT, k_words, k_scales, kb, offs, out):
 
         one = keep.tile([P, 8], F32, name="one")
         nc.gpsimd.memset(one[:], 1.0)
-        ones = keep.tile([P, P], F32, name="ones")
-        nc.scalar.activation(ones[:], one[:, 0:1].to_broadcast([P, P]), COPY)
 
         pool_scales = keep.tile([P, T], U8, name="pool_scales", align_bytes=64)
-        nc.sync.dma_start(pool_scales[P - SCALE_ROWS :, :].bitcast(I32), k_scales[0].bitcast(I32))
+        nc.scalar.dma_start(pool_scales[P - SCALE_ROWS :, :].bitcast(I32), k_scales[0].bitcast(I32))
         nc.sync.dma_start(offsets[:], offs)
         nc.vector.memset(pool_scales[: P - SCALE_ROWS, :].bitcast(I32), 0)
 
         pool_bias = keep.tile([P, T], F32, name="pool_bias")
-        nc.sync.dma_start(pool_bias[P - B :, SEG:], kb[0].rearrange("(b t) -> b t", b=B))
+        nc.scalar.dma_start(pool_bias[P - B :, SEG:], kb[0].rearrange("(b t) -> b t", b=B))
         nc.gpsimd.memset(pool_bias[: P - B, SEG:], 0.0)
+
+        ones = keep.tile([P, P], F32, name="ones")
+        nc.scalar.activation(ones[:], one[:, 0:1].to_broadcast([P, P]), COPY)
 
         raws, pool_words = [], []
         for b in range(B):

@@ -51,12 +51,13 @@ def tile_attend_sddmm_kb_seg_kernel(tc, qT, k_words, k_scales, kb, offs, out):
         nc.gpsimd.memset(one[:], 1.0)
 
         pool_scales = keep.tile([P, T], U8, name="pool_scales", align_bytes=64)
-        nc.scalar.dma_start(pool_scales[P - SCALE_ROWS :, :].bitcast(I32), k_scales[0].bitcast(I32))
+        nc.sync.dma_start(pool_scales[P - SCALE_ROWS :, :].bitcast(I32), k_scales[0].bitcast(I32))
         nc.sync.dma_start(offsets[:], offs)
         nc.vector.memset(pool_scales[: P - SCALE_ROWS, :].bitcast(I32), 0)
 
         pool_bias = keep.tile([P, T], F32, name="pool_bias")
-        nc.scalar.dma_start(pool_bias[P - B :, SEG:], kb[0].rearrange("(b t) -> b t", b=B))
+        for b in range(B):
+            nc.scalar.dma_start(pool_bias[P - B + b : P - B + b + 1, SEG:], kb[0:1, segs[b]])
         nc.gpsimd.memset(pool_bias[: P - B, SEG:], 0.0)
 
         ones = keep.tile([P, P], F32, name="ones")

@@ -174,8 +174,11 @@ def tile_attend_sddmm_kb_seg_kernel(tc, qT, k_words, k_scales, kb, offs, out):
             nc.vector.tensor_copy(words[b][:], pool_words[b][:].indirect(entries[b]))
         query1 = quantise("1", rounded[1], placed("q_words1", [P, NQ], U32, 24))
         acc = {}
-        for j in range(2):
-            acc[0, j] = product(f"acc0{j}", j, query0[j], words[0][:], key_scales[0])
+        first = [
+            product(f"acc00{h}", 5 * h, query0[0], words[0][:, halves[h]], key_scales[0][:, halves[h]])
+            for h in range(2)
+        ]
+        acc[0, 1] = product("acc01", 1, query0[1], words[0][:], key_scales[0])
         acc[1, 0] = product("acc10", 2, query1[0], words[1][:], key_scales[1])
         last = [
             product(f"acc11{h}", 3 + h, query1[1], words[1][:, halves[h]], key_scales[1][:, halves[h]])
@@ -186,7 +189,7 @@ def tile_attend_sddmm_kb_seg_kernel(tc, qT, k_words, k_scales, kb, offs, out):
 
         for h in range(2):
             score = keep.tile([P, HALF], F32, name=f"score00{h}")
-            nc.vector.tensor_tensor(score[:], acc[0, 0][:, halves[h]], bias0[:, halves[h]], ADD)
+            nc.vector.tensor_tensor(score[:], first[h][:], bias0[:, halves[h]], ADD)
             nc.scalar.activation(row00[:].indirect(half_entries(0, h)), score[:], COPY)
         store(0, 0, row00)
         score01 = keep.tile([P, N], F32, name="score01")

@@ -115,13 +115,13 @@ def tile_attend_sddmm_kb_seg_kernel(tc, qT, k_words, k_scales, kb, offs, out):
             return turned
 
         def bias_columns(b, turned, columns):
-            nc.scalar.copy(columns, turned[:, :, P - B + b])
+            nc.scalar.copy(columns, turned[:, :, P - B + b : P - B + b + 1].to_broadcast([P, 4, P]))
             return columns
 
         def spread_bias(b, columns, bank):
             spread = psum.tile([P, 4, P], F32, name=f"spread{b}", offset=bank * BANK)
             for c in range(4):
-                nc.tensor.transpose(spread[:, c, :], columns[:, c : c + 1].to_broadcast([P, P]), ident[:])
+                nc.tensor.transpose(spread[:, c, :], columns[:, c, :], ident[:])
             return spread
 
         def keep_bias(b, spread, bias):
@@ -154,8 +154,8 @@ def tile_attend_sddmm_kb_seg_kernel(tc, qT, k_words, k_scales, kb, offs, out):
         for b in range(B):
             gather_bias(b, picked_bias[b])
             turned.append(turn_bias(b, picked_bias[b], 4 + b))
-        columns = [bias_columns(0, turned[0], keep.tile([P, 4], F32, name="columns0")[:])]
-        columns.append(bias_columns(1, turned[1], keep.tile([P, 4], F32, name="columns1")[:]))
+        columns = [bias_columns(0, turned[0], keep.tile([P, 4, P], F32, name="columns0")[:])]
+        columns.append(bias_columns(1, turned[1], keep.tile([P, 4, P], F32, name="columns1")[:]))
         spread = [spread_bias(b, columns[b], 6 + b) for b in range(B)]
         bias0 = keep_bias(0, spread[0], keep.tile([P, N], F32, name="key_bias0"))
         bias1 = keep_bias(1, spread[1], keep.tile([P, N], F32, name="key_bias1"))

from contextlib import ExitStack

import concourse.mybir as mybir

B, N, T, D, NQ = 2, 512, 2048, 512, 256
P = 128
PACK = 4
SEG = T // B
HALF = N // 2
ZERO_COLS = SEG // 2
LIST_COLS = N // 16
SCALE_ROWS = D // 32
FLOPS = 2 * B * NQ * N * D

F32 = mybir.dt.float32
BF16 = mybir.dt.bfloat16
I32 = mybir.dt.int32
U32 = mybir.dt.uint32
U16 = mybir.dt.uint16
U8 = mybir.dt.uint8
FP8X4 = mybir.dt.float8_e4m3fn_x4
COPY = mybir.ActivationFunctionType.Copy
ADD = mybir.AluOpType.add
MULT = mybir.AluOpType.mult

KIB = 1024
BANK = 2 * KIB


def tile_attend_sddmm_kb_seg_kernel(tc, qT, k_words, k_scales, kb, offs, out):
    nc = tc.nc
    with ExitStack() as ctx:
        keep = ctx.enter_context(tc.tile_pool(name="keep", bufs=1))
        shared = ctx.enter_context(tc.tile_pool(name="shared", bufs=1))
        psum = ctx.enter_context(tc.psum_pool(name="psum", bufs=1))

        def placed(name, shape, dtype, kib):
            return shared.tile(shape, dtype, name=name, offset=int(kib * KIB), align_bytes=64)

        offsets = keep.tile([P, B * LIST_COLS], U16, name="offsets")
        entries = [offsets[:, b * LIST_COLS : (b + 1) * LIST_COLS] for b in range(B)]
        halves = [slice(h * HALF, (h + 1) * HALF) for h in range(2)]
        segs = [slice(b * SEG, (b + 1) * SEG) for b in range(B)]
        all_words = k_words[0].rearrange("p n t -> p (n t)").bitcast(I32)

        def half_entries(b, h):
            first = b * LIST_COLS + h * LIST_COLS // 2
            return offsets[:, first : first + LIST_COLS // 2]

        one = keep.tile([P, 8], F32, name="one")
        nc.gpsimd.memset(one[:], 1.0)

        pool_scales = keep.tile([P, T], U8, name="pool_scales", align_bytes=64)
        nc.sync.dma_start(pool_scales[P - SCALE_ROWS :, :].bitcast(I32), k_scales[0].bitcast(I32))
        nc.sync.dma_start(offsets[:], offs)
        nc.vector.memset(pool_scales[: P - SCALE_ROWS, :].bitcast(I32), 0)

        pool_bias = keep.tile([P, T], F32, name="pool_bias")
        for b in range(B):
            nc.scalar.dma_start(pool_bias[P - B + b : P - B + b + 1, SEG:], kb[0:1, segs[b]])
        nc.gpsimd.memset(pool_bias[: P - B, SEG:], 0.0)

        ones = keep.tile([P, P], F32, name="ones")
        nc.scalar.activation(ones[:], one[:, 0:1].to_broadcast([P, P]), COPY)

        raws, pool_words = [], []
        for b in range(B):
            raws.append(placed(f"raw{b}", [P, PACK, NQ], F32, 48 + 4 * b))
            nc.sync.dma_start(raws[b][:], qT[b].rearrange("(p j) w -> p j w", j=PACK))
            pool_words.append(keep.tile([P, (b + 1) * SEG], U32, name=f"pool_words{b}"))
            nc.sync.dma_start(pool_words[b][:, segs[b]].bitcast(I32), all_words[:, segs[b]])

        row00 = keep.tile([P, SEG], F32, name="row00")
        nc.gpsimd.memset(row00[:], 0.0)
        ident = keep.tile([P, P], F32, name="ident")
        nc.gpsimd.affine_select(
            out=ident[:],
            in_=ones[:],
            compare_op=mybir.AluOpType.is_equal,
            fill=0.0,
            base=0,
            pattern=[[-1, P]],
            channel_multiplier=1,
        )

        picked_scales = keep.tile([P, B * N], U8, name="picked_scales", align_bytes=64)
        nc.vector.tensor_copy(picked_scales[:], pool_scales[:].indirect(offsets[:]))
        planes = keep.tile([P, B * N], U8, name="planes", align_bytes=64)
        for r in range(4):
            nc.sync.dma_start(
                planes[r:P:32, :].bitcast(I32),
                picked_scales[P - SCALE_ROWS + r : P : 4, :].bitcast(I32),
            )
        key_scales = [planes[:, b * N : (b + 1) * N] for b in range(B)]

        def round_queries(rounded, raw):
            nc.gpsimd.tensor_scalar(rounded[:], raw[:].rearrange("p j w -> p w j"), 1.0, 0.0, MULT, ADD)

        def quantise(name, rounded, q_words):
            q_scales = keep.tile([P, NQ], U8, name=f"q_scales{name}", align_bytes=64)
            nc.vector.quantize_mx(
                out=q_words[:].bitcast(FP8X4),
                scales=q_scales[:],
                in_=rounded[:].rearrange("p w j -> p (w j)"),
            )
            return [(q_words[:, j * P : (j + 1) * P], q_scales[:, j * P : (j + 1) * P]) for j in range(2)]

        def gather_bias(b, picked):
            nc.scalar.activation(picked[:], pool_bias[:, (1 - b) * SEG :].indirect(entries[b]), COPY)

        def turn_bias(b, picked, bank):
            turned = psum.tile([P, 4, P], F32, name=f"turned{b}", offset=bank * BANK)
            for c in range(4):
                nc.tensor.transpose(turned[:, c, :], picked[:, c * P : (c + 1) * P], ident[:])
            return turned

        def bias_columns(b, turned, columns):
            nc.scalar.copy(columns, turned[:, :, P - B + b : P - B + b + 1].to_broadcast([P, 4, P]))
            return columns

        def spread_bias(b, columns, bank):
            spread = psum.tile([P, 4, P], F32, name=f"spread{b}", offset=bank * BANK)
            for c in range(4):
                nc.tensor.transpose(spread[:, c, :], columns[:, c, :], ident[:])
            return spread

        def keep_bias(b, spread, bias):
            nc.scalar.copy(bias[:], spread[:].rearrange("q c p -> q (c p)"))
            return bias

        def product(name, bank, query, words, scales):
            acc = psum.tile([P, words.shape[1]], F32, name=name, offset=bank * BANK)
            nc.tensor.matmul_mx(
                out=acc[:],
                lhsT=query[0].bitcast(FP8X4),
                lhsT_scale=query[1],
                rhs=words.bitcast(FP8X4),
                rhs_scale=scales,
                start=True,
                stop=True,
            )
            return acc

        def store(b, j, row):
            nc.sync.dma_start(out[b, j * P : (j + 1) * P, segs[b]], row[:, segs[b]])

        rounded = []
        for b, raw in enumerate(raws):
            rounded.append(placed(f"rounded{b}", [P, NQ, PACK], BF16, 40 - 36 * b))
            round_queries(rounded[b], raw)

        picked_bias = [keep.tile([P, N], F32, name="picked_bias0"), keep.tile([P, N], F32, name="picked_bias1")]
        turned = []
        for b in range(B):
            gather_bias(b, picked_bias[b])
            turned.append(turn_bias(b, picked_bias[b], 4 + b))
        columns = [bias_columns(0, turned[0], keep.tile([P, 4, P], F32, name="columns0")[:])]
        columns.append(bias_columns(1, turned[1], keep.tile([P, 4, P], F32, name="columns1")[:]))
        spread = [spread_bias(b, columns[b], 6 + b) for b in range(B)]
        bias0 = keep_bias(0, spread[0], keep.tile([P, N], F32, name="key_bias0"))
        bias1 = keep_bias(1, spread[1], keep.tile([P, N], F32, name="key_bias1"))

        query0 = quantise("0", rounded[0], keep.tile([P, NQ], U32, name="q_words0", align_bytes=64))
        zeros = placed("zeros", [P, ZERO_COLS], F32, 48)
        nc.vector.memset(zeros[:], 0.0)
        for b in range(B):
            for j in range(NQ // P):
                nc.sync.dma_start(
                    out[b, j * P : (j + 1) * P, segs[1 - b]].rearrange("p (r c) -> p r c", c=ZERO_COLS),
                    zeros[:].unsqueeze(1).to_broadcast([P, SEG // ZERO_COLS, ZERO_COLS]),
                )
        words = [placed("words0", [P, N], U32, 39), placed("words1", [P, N], U32, 41)]
        for b in range(B):
            nc.vector.tensor_copy(words[b][:], pool_words[b][:].indirect(entries[b]))
        query1 = quantise("1", rounded[1], placed("q_words1", [P, NQ], U32, 24))
        acc = {}
        first = [
            product(f"acc00{h}", 5 * h, query0[0], words[0][:, halves[h]], key_scales[0][:, halves[h]])
            for h in range(2)
        ]
        acc[0, 1] = product("acc01", 1, query0[1], words[0][:], key_scales[0])
        acc[1, 0] = product("acc10", 2, query1[0], words[1][:], key_scales[1])
        last = [
            product(f"acc11{h}", 3 + h, query1[1], words[1][:, halves[h]], key_scales[1][:, halves[h]])
            for h in range(2)
        ]
        row10 = placed("row10", [P, T], F32, 5.5)
        nc.gpsimd.memset(row10[:, segs[1]], 0.0)

        for h in range(2):
            score = keep.tile([P, HALF], F32, name=f"score00{h}")
            nc.vector.tensor_tensor(score[:], first[h][:], bias0[:, halves[h]], ADD)
            nc.scalar.activation(row00[:].indirect(half_entries(0, h)), score[:], COPY)
        store(0, 0, row00)
        score01 = keep.tile([P, N], F32, name="score01")
        nc.vector.tensor_tensor(score01[:], acc[0, 1][:], bias0[:], ADD)
        score10 = keep.tile([P, N], F32, name="score10")
        nc.vector.tensor_copy(score10[:], acc[1, 0][:])
        score11 = keep.tile([P, N], F32, name="score11")
        nc.vector.tensor_copy(score11[:, halves[0]], last[0][:])
        nc.vector.tensor_tensor(row10[:].indirect(entries[1]), score10[:], bias1[:], ADD)
        store(1, 0, row10)

        nc.scalar.copy(score11[:, halves[1]], last[1][:])
        row01 = placed("row01", [P, SEG], F32, 42.5)
        nc.gpsimd.memset(row01[:], 0.0)
        row11 = placed("row11", [P, T], F32, 24)
        nc.gpsimd.memset(row11[:, segs[1]], 0.0)
        for h in range(2):
            nc.scalar.activation(row01[:].indirect(half_entries(0, h)), score01[:, halves[h]], COPY)
        store(0, 1, row01)
        nc.vector.tensor_tensor(row11[:].indirect(entries[1]), score11[:], bias1[:], ADD)
        store(1, 1, row11)
